import numpy as np
import ml_dtypes


def mxq(x, axis, fmt="e4m3"):
    dtype, down = {"e4m3": (ml_dtypes.float8_e4m3fn, 7), "e5m2": (ml_dtypes.float8_e5m2, 14)}[fmt]
    v = np.moveaxis(np.asarray(x, np.float32).astype(ml_dtypes.bfloat16).astype(np.float64), axis, -1)
    blocks = v.reshape(v.shape[:-1] + (-1, 32))
    amax = np.abs(blocks).max(-1, keepdims=True)
    byte = np.maximum(np.where(amax > 0, np.frexp(amax)[1] - 1 + 127, 0) - down, 1)
    scale = np.exp2(byte - 127.0)
    codes = (blocks / scale).astype(np.float32).astype(dtype).astype(np.float64)
    return np.moveaxis((codes * scale).reshape(v.shape), -1, axis)


WIDE = False


def mx_kscale(k):
    if not WIDE:
        return np.ones(k)
    levels = np.array([10, -10, 5, -5, 0])
    if k % 512:
        return np.exp2(np.random.permutation(np.resize(levels, k // 32))).repeat(32)
    a = np.empty((k // 512, 16))
    for p in range(k // 512):
        a[p, :8] = np.random.permutation(np.resize(levels, 8))
        for g in range(8):
            far = levels[np.abs(levels - a[p, g]) >= 10]
            a[p, g + 8] = far[np.random.randint(len(far))]
    return np.exp2(a.ravel()).repeat(32)


def f64(x):
    return np.asarray(x).astype(np.float64)


def striped8(idx):
    return np.concatenate([v.reshape(-1, 16).T for v in idx]).astype(np.uint16)


def unstriped8(offs):
    return np.stack([offs[16 * g:16 * g + 16].T.reshape(-1) for g in range(8)]).astype(np.int64)


K, M, T, S = 2048, 1024, 1024, 512


def setup_inputs():
    n = np.random.standard_normal
    s = mx_kscale(K)[:, None]
    return {
        "x": (n((K, S)) * s).astype(np.float32),
        "w": (n((K, M)) / np.sqrt(K) / s).astype(np.float32),
        "b": (0.3 * n(1024)).astype(np.float32),
        "wgo": np.repeat(np.random.uniform(0.5, 2.0, (8, S)), 16, axis=0).astype(np.float32),
        "offs": striped8(np.stack([np.random.permutation(T)[:S] for _ in range(8)])),
    }


def reference(x, w, b, wgo, offs):
    x_ = mxq(f64(x), 0, "e4m3")
    w_ = mxq(f64(w), 0, "e4m3")
    y = w_.T @ x_
    place = unstriped8(offs)[np.arange(M) % 128 // 16]
    out = np.zeros((M, T))
    out[np.arange(M)[:, None], place] = f64(wgo)[np.arange(M) % 128] * (y + f64(b)[:, None])
    return out

@@ -1,0 +1,178 @@
+from contextlib import ExitStack
+
+import concourse.mybir as mybir
+from concourse.masks import make_identity
+
+K, M, T, S = 2048, 1024, 1024, 512
+FLOPS = 2 * K * M * S
+
+F32 = mybir.dt.float32
+BF16 = mybir.dt.bfloat16
+U32 = mybir.dt.uint32
+U16 = mybir.dt.uint16
+U8 = mybir.dt.uint8
+FP8X4 = mybir.dt.float8_e4m3fn_x4
+IDENTITY = mybir.ActivationFunctionType.Identity
+MULT = mybir.AluOpType.mult
+
+P = 128
+PACK = 4
+K_PASS = P * PACK
+PASSES = K // K_PASS
+BLOCKS = M // P
+HALF = S // 2
+WINDOWS = 6
+
+
+def interleave(copy, grouped, raw):
+    copy(
+        out=grouped.rearrange("p (c i j) -> p c j i", i=4, j=PACK),
+        in_=raw.rearrange("p j (c i) -> p c j i", i=4),
+    )
+
+
+def tile_list_hscat_bias_kernel(tc, x, w, b, wgo, offs, out):
+    nc = tc.nc
+    with ExitStack() as ctx:
+        keep = ctx.enter_context(tc.tile_pool(name="keep", bufs=1))
+        psum = ctx.enter_context(tc.psum_pool(name="psum", bufs=4))
+        psum_b = ctx.enter_context(tc.psum_pool(name="psum_b", bufs=1))
+
+        offsets = keep.tile([P, S // 16], U16, name="offsets")
+        weights = keep.tile([P, S], F32, name="weights")
+        b_rows = keep.tile([P, P], F32, name="b_rows")
+        ident = keep.tile([P, P], F32, name="ident")
+        b_cols = keep.tile([P, BLOCKS], F32, name="b_cols")
+        windows = [keep.tile([P, T], F32, name=f"window{i}") for i in range(WINDOWS)]
+        x_raw = [keep.tile([P, PACK, S], F32, name=f"x_raw{a}") for a in range(PASSES)]
+        w_raw = [[keep.tile([P, PACK, P], F32, name=f"w_raw{q}_{a}") for a in range(PASSES)] for q in range(BLOCKS)]
+        x_codes = keep.tile([P, PASSES, S], U32, align_bytes=64, name="x_codes")
+        x_scales = keep.tile([P, PASSES, S], U8, align_bytes=64, name="x_scales")
+        x_grouped = [keep.tile([P, S * PACK], BF16, align_bytes=64, name=f"x_grouped{a}") for a in range(PASSES)]
+        w_codes = [keep.tile([P, PASSES, P], U32, align_bytes=64, name=f"w_codes{q}") for q in range(BLOCKS)]
+        w_scales = [keep.tile([P, PASSES, P], U8, align_bytes=64, name=f"w_scales{q}") for q in range(BLOCKS)]
+        w_grouped = [keep.tile([P, PASSES, P * PACK], BF16, align_bytes=64, name=f"w_grouped{q}") for q in range(BLOCKS)]
+
+        def load_x(a):
+            rows = x[a * K_PASS : (a + 1) * K_PASS, :]
+            nc.sync.dma_start(out=x_raw[a][:], in_=rows.rearrange("(p j) c -> p j c", j=PACK))
+
+        def load_w(q, a):
+            rows = w[a * K_PASS : (a + 1) * K_PASS, q * P : (q + 1) * P]
+            nc.sync.dma_start(out=w_raw[q][a][:], in_=rows.rearrange("(p j) c -> p j c", j=PACK))
+
+        def group_x(a, h, copy):
+            interleave(
+                copy,
+                x_grouped[a][:, h * HALF * PACK : (h + 1) * HALF * PACK],
+                x_raw[a][:, :, h * HALF : (h + 1) * HALF],
+            )
+
+        def quantize_x(a, h):
+            cols = slice(h * HALF, (h + 1) * HALF)
+            nc.vector.quantize_mx(
+                out=x_codes[:, a, cols].bitcast(FP8X4),
+                scales=x_scales[:, a, cols],
+                in_=x_grouped[a][:, h * HALF * PACK : (h + 1) * HALF * PACK],
+            )
+
+        def group_w(q, a, copy):
+            interleave(copy, w_grouped[q][:, a, :], w_raw[q][a][:])
+
+        def quantize_w(q, a0, a1):
+            nc.vector.quantize_mx(
+                out=w_codes[q][:, a0:a1, :].rearrange("p a c -> p (a c)").bitcast(FP8X4),
+                scales=w_scales[q][:, a0:a1, :].rearrange("p a c -> p (a c)"),
+                in_=w_grouped[q][:, a0:a1, :].rearrange("p a c -> p (a c)"),
+            )
+
+        def multiply(q, a0, a1, acc):
+            for a in range(a0, a1):
+                nc.tensor.matmul_mx(
+                    out=acc[:],
+                    lhsT=w_codes[q][:, a, :].bitcast(FP8X4),
+                    lhsT_scale=w_scales[q][:, a, :],
+                    rhs=x_codes[:, a, :].bitcast(FP8X4),
+                    rhs_scale=x_scales[:, a, :],
+                    start=(a == 0),
+                    stop=(a == PASSES - 1),
+                )
+
+        def add_bias(q, h, acc, y):
+            cols = slice(h * HALF, (h + 1) * HALF)
+            nc.scalar.activation(out=y, in_=acc[:, cols], func=IDENTITY, bias=b_cols[:, q : q + 1])
+
+        def place(q, h, y):
+            cols = slice(h * HALF, (h + 1) * HALF)
+            nc.vector.tensor_tensor(
+                windows[q % WINDOWS][:].indirect(offsets[:, h * HALF // 16 : (h + 1) * HALF // 16]),
+                y,
+                weights[:, cols],
+                MULT,
+            )
+
+        def store(q):
+            nc.sync.dma_start(out=out[q * P : (q + 1) * P, :], in_=windows[q % WINDOWS][:])
+
+        nc.gpsimd.memset(b_rows[:], 0.0)
+        make_identity(nc, ident[:])
+        nc.sync.dma_start(out=b_rows[0:BLOCKS, :], in_=b.rearrange("(c p) -> c p", p=P))
+        nc.sync.dma_start(offsets[:], offs)
+        for a in range(PASSES):
+            load_x(a)
+            if a < 2:
+                load_w(0, a)
+        load_w(0, 2)
+        load_w(0, 3)
+        nc.sync.dma_start(out=weights[:], in_=wgo)
+        for q in range(1, BLOCKS):
+            for a in range(PASSES):
+                load_w(q, a)
+        for i in range(WINDOWS):
+            (nc.vector if i < 4 else nc.gpsimd).memset(windows[i][:], 0.0)
+
+        vcopy, scopy = nc.vector.tensor_copy, nc.scalar.copy
+        acc = psum.tile([P, S], F32, name="acc")
+        bt = psum_b.tile([P, P], F32, name="bt")
+        nc.tensor.transpose(bt[:], b_rows[:], ident[:])
+        for a in range(PASSES):
+            group_x(a, 1, scopy)
+            group_x(a, 0, vcopy)
+            if a < 2:
+                group_w(0, a, scopy)
+            if a == 0:
+                scopy(out=b_cols[:], in_=bt[:, 0:BLOCKS])
+            quantize_x(a, 0)
+            quantize_x(a, 1)
+            if a < 2:
+                quantize_w(0, a, a + 1)
+                multiply(0, a, a + 1, acc)
+        group_w(0, 2, scopy)
+        group_w(0, 3, vcopy)
+        quantize_w(0, 2, 3)
+        quantize_w(0, 3, 4)
+        multiply(0, 2, 4, acc)
+        passes = [(1 + i // PASSES, i % PASSES) for i in range((BLOCKS - 1) * PASSES)]
+        accs = [acc]
+        for u in range(2 * BLOCKS):
+            q, h = divmod(u, 2)
+            n = {0: 0, 1: PASSES}.get(u, PASSES // 2)
+            ahead, passes = passes[:n], passes[n:]
+            for nq, a in ahead:
+                group_w(nq, a, scopy)
+                if a % 2 == 1:
+                    quantize_w(nq, a - 1, a + 1)
+            if ahead:
+                nq, a = ahead[-1]
+                y = w_raw[nq][a][:, 0:2, :].rearrange("p j c -> p (j c)")
+            else:
+                own = keep.tile([P, HALF], F32, name=f"y{u}")
+                y = own[:]
+            add_bias(q, h, accs[q], y)
+            place(q, h, y)
+            for nq, a in ahead:
+                if a == 0:
+                    accs.append(psum.tile([P, S], F32, name="acc"))
+                multiply(nq, a, a + 1, accs[nq])
+            if h == 1:
+                store(q)

@@ -35,144 +35,153 @@ def tile_list_hscat_bias_kernel(tc, x, w, b, wgo, offs, out):
     nc = tc.nc
     with ExitStack() as ctx:
         keep = ctx.enter_context(tc.tile_pool(name="keep", bufs=1))
-        psum = ctx.enter_context(tc.psum_pool(name="psum", bufs=4))
+        psum = ctx.enter_context(tc.psum_pool(name="psum", bufs=7))
         psum_b = ctx.enter_context(tc.psum_pool(name="psum_b", bufs=1))
 
         offsets = keep.tile([P, S // 16], U16, name="offsets")
         weights = keep.tile([P, S], F32, name="weights")
         b_rows = keep.tile([P, P], F32, name="b_rows")
+        b_load = keep.tile([BLOCKS, P], F32, name="b_load")
         ident = keep.tile([P, P], F32, name="ident")
         b_cols = keep.tile([P, BLOCKS], F32, name="b_cols")
         windows = [keep.tile([P, T], F32, name=f"window{i}") for i in range(WINDOWS)]
-        x_raw = [keep.tile([P, PACK, S], F32, name=f"x_raw{a}") for a in range(PASSES)]
-        w_raw = [[keep.tile([P, PACK, P], F32, name=f"w_raw{q}_{a}") for a in range(PASSES)] for q in range(BLOCKS)]
         x_codes = keep.tile([P, PASSES, S], U32, align_bytes=64, name="x_codes")
         x_scales = keep.tile([P, PASSES, S], U8, align_bytes=64, name="x_scales")
-        x_grouped = [keep.tile([P, S * PACK], BF16, align_bytes=64, name=f"x_grouped{a}") for a in range(PASSES)]
         w_codes = [keep.tile([P, PASSES, P], U32, align_bytes=64, name=f"w_codes{q}") for q in range(BLOCKS)]
         w_scales = [keep.tile([P, PASSES, P], U8, align_bytes=64, name=f"w_scales{q}") for q in range(BLOCKS)]
-        w_grouped = [keep.tile([P, PASSES, P * PACK], BF16, align_bytes=64, name=f"w_grouped{q}") for q in range(BLOCKS)]
 
-        def load_x(a):
-            rows = x[a * K_PASS : (a + 1) * K_PASS, :]
-            nc.sync.dma_start(out=x_raw[a][:], in_=rows.rearrange("(p j) c -> p j c", j=PACK))
+        raw, grouped = {}, {}
 
-        def load_w(q, a):
-            rows = w[a * K_PASS : (a + 1) * K_PASS, q * P : (q + 1) * P]
-            nc.sync.dma_start(out=w_raw[q][a][:], in_=rows.rearrange("(p j) c -> p j c", j=PACK))
+        def declare(piece):
+            name, c0, c1 = piece
+            raw[piece] = [keep.tile([P, PACK, c1 - c0], F32, name=f"raw_{name}{c0}_{a}") for a in range(PASSES)]
+            grouped[piece] = keep.tile([P, PASSES, (c1 - c0) * PACK], BF16, align_bytes=64, name=f"grouped_{name}{c0}")
 
-        def group_x(a, h, copy):
-            interleave(
-                copy,
-                x_grouped[a][:, h * HALF * PACK : (h + 1) * HALF * PACK],
-                x_raw[a][:, :, h * HALF : (h + 1) * HALF],
-            )
+        def load(piece, a):
+            name, c0, c1 = piece
+            rows = (x if name == "x" else w)[a * K_PASS : (a + 1) * K_PASS, c0:c1]
+            nc.sync.dma_start(out=raw[piece][a][:], in_=rows.rearrange("(p j) c -> p j c", j=PACK))
 
-        def quantize_x(a, h):
-            cols = slice(h * HALF, (h + 1) * HALF)
-            nc.vector.quantize_mx(
-                out=x_codes[:, a, cols].bitcast(FP8X4),
-                scales=x_scales[:, a, cols],
-                in_=x_grouped[a][:, h * HALF * PACK : (h + 1) * HALF * PACK],
-            )
+        def group(piece, a, copy, i0, i1):
+            interleave(copy, grouped[piece][:, a, i0 * PACK : i1 * PACK], raw[piece][a][:, :, i0:i1])
 
-        def group_w(q, a, copy):
-            interleave(copy, w_grouped[q][:, a, :], w_raw[q][a][:])
-
-        def quantize_w(q, a0, a1):
-            nc.vector.quantize_mx(
-                out=w_codes[q][:, a0:a1, :].rearrange("p a c -> p (a c)").bitcast(FP8X4),
-                scales=w_scales[q][:, a0:a1, :].rearrange("p a c -> p (a c)"),
-                in_=w_grouped[q][:, a0:a1, :].rearrange("p a c -> p (a c)"),
-            )
-
-        def multiply(q, a0, a1, acc):
-            for a in range(a0, a1):
-                nc.tensor.matmul_mx(
-                    out=acc[:],
-                    lhsT=w_codes[q][:, a, :].bitcast(FP8X4),
-                    lhsT_scale=w_scales[q][:, a, :],
-                    rhs=x_codes[:, a, :].bitcast(FP8X4),
-                    rhs_scale=x_scales[:, a, :],
-                    start=(a == 0),
-                    stop=(a == PASSES - 1),
+        def quantize(piece, a0, a1):
+            name, c0, c1 = piece
+            if name == "x":
+                for a in range(a0, a1):
+                    nc.vector.quantize_mx(
+                        out=x_codes[:, a, c0:c1].bitcast(FP8X4),
+                        scales=x_scales[:, a, c0:c1],
+                        in_=grouped[piece][:, a, :],
+                    )
+            else:
+                q = c0 // P
+                nc.vector.quantize_mx(
+                    out=w_codes[q][:, a0:a1, :].rearrange("p a c -> p (a c)").bitcast(FP8X4),
+                    scales=w_scales[q][:, a0:a1, :].rearrange("p a c -> p (a c)"),
+                    in_=grouped[piece][:, a0:a1, :].rearrange("p a c -> p (a c)"),
                 )
 
-        def add_bias(q, h, acc, y):
-            cols = slice(h * HALF, (h + 1) * HALF)
-            nc.scalar.activation(out=y, in_=acc[:, cols], func=IDENTITY, bias=b_cols[:, q : q + 1])
+        accs = {}
 
-        def place(q, h, y):
-            cols = slice(h * HALF, (h + 1) * HALF)
-            nc.vector.tensor_tensor(
-                windows[q % WINDOWS][:].indirect(offsets[:, h * HALF // 16 : (h + 1) * HALF // 16]),
-                y,
-                weights[:, cols],
-                MULT,
+        def multiply(unit, a):
+            q, c0, c1 = unit
+            if a == 0:
+                accs[unit] = psum.tile([P, S], F32, name="acc")
+            nc.tensor.matmul_mx(
+                out=accs[unit][:, 0 : c1 - c0],
+                lhsT=w_codes[q][:, a, :].bitcast(FP8X4),
+                lhsT_scale=w_scales[q][:, a, :],
+                rhs=x_codes[:, a, c0:c1].bitcast(FP8X4),
+                rhs_scale=x_scales[:, a, c0:c1],
+                start=(a == 0),
+                stop=(a == PASSES - 1),
             )
 
-        def store(q):
-            nc.sync.dma_start(out=out[q * P : (q + 1) * P, :], in_=windows[q % WINDOWS][:])
+        placed = [0] * BLOCKS
+
+        def place(unit, y):
+            q, c0, c1 = unit
+            nc.scalar.activation(out=y, in_=accs[unit][:, 0 : c1 - c0], func=IDENTITY, bias=b_cols[:, q : q + 1])
+            nc.vector.tensor_tensor(
+                windows[q % WINDOWS][:].indirect(offsets[:, c0 // 16 : c1 // 16]),
+                y,
+                weights[:, c0:c1],
+                MULT,
+            )
+            placed[q] = placed[q] + c1 - c0
+            if placed[q] == S:
+                nc.sync.dma_start(out=out[q * P : (q + 1) * P, :], in_=windows[q % WINDOWS][:])
+
+        def place_own(unit):
+            q, c0, c1 = unit
+            own = keep.tile([P, c1 - c0], F32, name=f"y{q}_{c0}")
+            place(unit, own[:])
+
+        x_first = ("x", 0, HALF)
+        blocks = [("w", q * P, (q + 1) * P) for q in range(BLOCKS)]
+        fine = [(0, 2), (2, 3), (3, 4)]
+        pairs = [(0, 2), (2, 4)]
+        whole = [(0, 4)]
+        first_units, first_held = [(0, 0, P)], [(0, P, HALF)]
+        steps = [(blocks[q], [(q, 0, P)], [(q, P, HALF)], fine) for q in (1, 2)]
+        for c0 in (HALF, HALF + P):
+            steps.append((("x", c0, c0 + P), [(0, c0, c0 + P), (1, c0, c0 + P)], [(2, c0, c0 + P)], fine))
+        steps.extend([(blocks[q], [(q, 0, HALF)], [(q, HALF, S)], fine) for q in (3, 4)])
+        steps.extend([(blocks[q], [], [(q, 0, S)], pairs) for q in (5, 6, 7)])
+        for piece in [x_first, blocks[0]] + [step[0] for step in steps]:
+            declare(piece)
 
         nc.gpsimd.memset(b_rows[:], 0.0)
         make_identity(nc, ident[:])
-        nc.sync.dma_start(out=b_rows[0:BLOCKS, :], in_=b.rearrange("(c p) -> c p", p=P))
+        nc.sync.dma_start(out=b_load[:], in_=b.rearrange("(c p) -> c p", p=P))
         nc.sync.dma_start(offsets[:], offs)
         for a in range(PASSES):
-            load_x(a)
-            if a < 2:
-                load_w(0, a)
-        load_w(0, 2)
-        load_w(0, 3)
-        nc.sync.dma_start(out=weights[:], in_=wgo)
-        for q in range(1, BLOCKS):
+            load(x_first, a)
+            load(blocks[0], a)
+        for piece, units, held, splits in steps:
             for a in range(PASSES):
-                load_w(q, a)
+                load(piece, a)
+                if a == 1 and piece == blocks[1]:
+                    nc.sync.dma_start(out=weights[:, 0:HALF], in_=wgo[:, 0:HALF])
+                if a == 1 and piece[0:2] == ("x", HALF):
+                    nc.sync.dma_start(out=weights[:, HALF:S], in_=wgo[:, HALF:S])
         for i in range(WINDOWS):
-            (nc.vector if i < 4 else nc.gpsimd).memset(windows[i][:], 0.0)
+            (nc.vector if i < 6 else nc.gpsimd).memset(windows[i][:], 0.0)
 
         vcopy, scopy = nc.vector.tensor_copy, nc.scalar.copy
-        acc = psum.tile([P, S], F32, name="acc")
         bt = psum_b.tile([P, P], F32, name="bt")
+        scopy(out=b_rows[0:BLOCKS, :], in_=b_load[:])
         nc.tensor.transpose(bt[:], b_rows[:], ident[:])
+        scopy(out=b_cols[:], in_=bt[:, 0:BLOCKS])
         for a in range(PASSES):
-            group_x(a, 1, scopy)
-            group_x(a, 0, vcopy)
-            if a < 2:
-                group_w(0, a, scopy)
-            if a == 0:
-                scopy(out=b_cols[:], in_=bt[:, 0:BLOCKS])
-            quantize_x(a, 0)
-            quantize_x(a, 1)
-            if a < 2:
-                quantize_w(0, a, a + 1)
-                multiply(0, a, a + 1, acc)
-        group_w(0, 2, scopy)
-        group_w(0, 3, vcopy)
-        quantize_w(0, 2, 3)
-        quantize_w(0, 3, 4)
-        multiply(0, 2, 4, acc)
-        passes = [(1 + i // PASSES, i % PASSES) for i in range((BLOCKS - 1) * PASSES)]
-        accs = [acc]
-        for u in range(2 * BLOCKS):
-            q, h = divmod(u, 2)
-            n = {0: 0, 1: PASSES}.get(u, PASSES // 2)
-            ahead, passes = passes[:n], passes[n:]
-            for nq, a in ahead:
-                group_w(nq, a, scopy)
-                if a % 2 == 1:
-                    quantize_w(nq, a - 1, a + 1)
-            if ahead:
-                nq, a = ahead[-1]
-                y = w_raw[nq][a][:, 0:2, :].rearrange("p j c -> p (j c)")
-            else:
-                own = keep.tile([P, HALF], F32, name=f"y{u}")
-                y = own[:]
-            add_bias(q, h, accs[q], y)
-            place(q, h, y)
-            for nq, a in ahead:
-                if a == 0:
-                    accs.append(psum.tile([P, S], F32, name="acc"))
-                multiply(nq, a, a + 1, accs[nq])
-            if h == 1:
-                store(q)
+            group(x_first, a, scopy, P, HALF)
+            group(x_first, a, vcopy, 0, P)
+            group(blocks[0], a, scopy, 0, P)
+            quantize(x_first, a, a + 1)
+            quantize(blocks[0], a, a + 1)
+            for unit in first_units + first_held:
+                multiply(unit, a)
+        for unit in first_units:
+            place_own(unit)
+        waiting = first_held
+        on_vector = []
+        for piece, units, held, splits in steps:
+            width = piece[2] - piece[1]
+            for a0, a1 in splits:
+                for a in range(a0, a1):
+                    group(piece, a, vcopy if (piece[0:2], a) in on_vector else scopy, 0, width)
+                quantize(piece, a0, a1)
+                for a in range(a0, a1):
+                    for unit in units + held:
+                        multiply(unit, a)
+            last = raw[piece][2][:].rearrange("p j c -> p (j c)")
+            at = 0
+            for unit in waiting:
+                place(unit, last[:, at : at + unit[2] - unit[1]])
+                at = at + unit[2] - unit[1]
+            for unit in units:
+                place_own(unit)
+            waiting = held
+        for unit in waiting:
+            place_own(unit)

@@ -22,6 +22,7 @@ PASSES = K // K_PASS
 BLOCKS = M // P
 HALF = S // 2
 WINDOWS = 6
+HALVED = 4
 
 
 def interleave(copy, grouped, raw):
@@ -35,6 +36,7 @@ def tile_list_hscat_bias_kernel(tc, x, w, b, wgo, offs, out):
     nc = tc.nc
     with ExitStack() as ctx:
         keep = ctx.enter_context(tc.tile_pool(name="keep", bufs=1))
+        ring = ctx.enter_context(tc.tile_pool(name="ring", bufs=2))
         psum = ctx.enter_context(tc.psum_pool(name="psum", bufs=7))
         psum_b = ctx.enter_context(tc.psum_pool(name="psum_b", bufs=1))
 
@@ -49,38 +51,31 @@ def tile_list_hscat_bias_kernel(tc, x, w, b, wgo, offs, out):
         x_scales = keep.tile([P, PASSES, S], U8, align_bytes=64, name="x_scales")
         w_codes = [keep.tile([P, PASSES, P], U32, align_bytes=64, name=f"w_codes{q}") for q in range(BLOCKS)]
         w_scales = [keep.tile([P, PASSES, P], U8, align_bytes=64, name=f"w_scales{q}") for q in range(BLOCKS)]
+        x_raw = [keep.tile([P, PACK, S], F32, name=f"x_raw{a}") for a in range(PASSES)]
+        w_raw = [[keep.tile([P, PACK, P], F32, name=f"w_raw{q}_{a}") for a in range(PASSES)] for q in range(BLOCKS)]
+        x_grouped = [keep.tile([P, HALF * PACK], BF16, align_bytes=64, name=f"x_grouped{i}") for i in range(2)]
+        w_first = [keep.tile([P, P * PACK], BF16, align_bytes=64, name=f"w_first{a}") for a in range(PASSES)]
+        vcopy, scopy = nc.vector.tensor_copy, nc.scalar.copy
 
-        raw, grouped = {}, {}
+        def load_x(a):
+            rows = x[a * K_PASS : (a + 1) * K_PASS, :]
+            nc.sync.dma_start(out=x_raw[a][:], in_=rows.rearrange("(p j) c -> p j c", j=PACK))
 
-        def declare(piece):
-            name, c0, c1 = piece
-            raw[piece] = [keep.tile([P, PACK, c1 - c0], F32, name=f"raw_{name}{c0}_{a}") for a in range(PASSES)]
-            grouped[piece] = keep.tile([P, PASSES, (c1 - c0) * PACK], BF16, align_bytes=64, name=f"grouped_{name}{c0}")
+        def load_w(q, a):
+            rows = w[a * K_PASS : (a + 1) * K_PASS, q * P : (q + 1) * P]
+            nc.sync.dma_start(out=w_raw[q][a][:], in_=rows.rearrange("(p j) c -> p j c", j=PACK))
 
-        def load(piece, a):
-            name, c0, c1 = piece
-            rows = (x if name == "x" else w)[a * K_PASS : (a + 1) * K_PASS, c0:c1]
-            nc.sync.dma_start(out=raw[piece][a][:], in_=rows.rearrange("(p j) c -> p j c", j=PACK))
+        def quantize_x(a, c0, c1, grouped):
+            nc.vector.quantize_mx(
+                out=x_codes[:, a, c0:c1].bitcast(FP8X4), scales=x_scales[:, a, c0:c1], in_=grouped
+            )
 
-        def group(piece, a, copy, i0, i1):
-            interleave(copy, grouped[piece][:, a, i0 * PACK : i1 * PACK], raw[piece][a][:, :, i0:i1])
-
-        def quantize(piece, a0, a1):
-            name, c0, c1 = piece
-            if name == "x":
-                for a in range(a0, a1):
-                    nc.vector.quantize_mx(
-                        out=x_codes[:, a, c0:c1].bitcast(FP8X4),
-                        scales=x_scales[:, a, c0:c1],
-                        in_=grouped[piece][:, a, :],
-                    )
-            else:
-                q = c0 // P
-                nc.vector.quantize_mx(
-                    out=w_codes[q][:, a0:a1, :].rearrange("p a c -> p (a c)").bitcast(FP8X4),
-                    scales=w_scales[q][:, a0:a1, :].rearrange("p a c -> p (a c)"),
-                    in_=grouped[piece][:, a0:a1, :].rearrange("p a c -> p (a c)"),
-                )
+        def quantize_w(q, a0, a1, grouped):
+            nc.vector.quantize_mx(
+                out=w_codes[q][:, a0:a1, :].rearrange("p a c -> p (a c)").bitcast(FP8X4),
+                scales=w_scales[q][:, a0:a1, :].rearrange("p a c -> p (a c)"),
+                in_=grouped,
+            )
 
         accs = {}
 
@@ -98,90 +93,107 @@ def tile_list_hscat_bias_kernel(tc, x, w, b, wgo, offs, out):
                 stop=(a == PASSES - 1),
             )
 
-        placed = [0] * BLOCKS
+        def add_bias(unit, y, bias, i0, i1):
+            nc.scalar.activation(out=y[:, i0:i1], in_=accs[unit][:, i0:i1], func=IDENTITY, bias=bias)
 
         def place(unit, y):
             q, c0, c1 = unit
-            nc.scalar.activation(out=y, in_=accs[unit][:, 0 : c1 - c0], func=IDENTITY, bias=b_cols[:, q : q + 1])
             nc.vector.tensor_tensor(
                 windows[q % WINDOWS][:].indirect(offsets[:, c0 // 16 : c1 // 16]),
                 y,
                 weights[:, c0:c1],
                 MULT,
             )
-            placed[q] = placed[q] + c1 - c0
-            if placed[q] == S:
+            if c1 == S:
                 nc.sync.dma_start(out=out[q * P : (q + 1) * P, :], in_=windows[q % WINDOWS][:])
 
         def place_own(unit):
             q, c0, c1 = unit
             own = keep.tile([P, c1 - c0], F32, name=f"y{q}_{c0}")
+            add_bias(unit, own[:], b_cols[:, q : q + 1], 0, c1 - c0)
             place(unit, own[:])
-
-        x_first = ("x", 0, HALF)
-        blocks = [("w", q * P, (q + 1) * P) for q in range(BLOCKS)]
-        fine = [(0, 2), (2, 3), (3, 4)]
-        pairs = [(0, 2), (2, 4)]
-        whole = [(0, 4)]
-        first_units, first_held = [(0, 0, P)], [(0, P, HALF)]
-        steps = [(blocks[q], [(q, 0, P)], [(q, P, HALF)], fine) for q in (1, 2)]
-        for c0 in (HALF, HALF + P):
-            steps.append((("x", c0, c0 + P), [(0, c0, c0 + P), (1, c0, c0 + P)], [(2, c0, c0 + P)], fine))
-        steps.extend([(blocks[q], [(q, 0, HALF)], [(q, HALF, S)], fine) for q in (3, 4)])
-        steps.extend([(blocks[q], [], [(q, 0, S)], pairs) for q in (5, 6, 7)])
-        for piece in [x_first, blocks[0]] + [step[0] for step in steps]:
-            declare(piece)
 
         nc.gpsimd.memset(b_rows[:], 0.0)
         make_identity(nc, ident[:])
         nc.sync.dma_start(out=b_load[:], in_=b.rearrange("(c p) -> c p", p=P))
         nc.sync.dma_start(offsets[:], offs)
+        load_w(0, 0)
         for a in range(PASSES):
-            load(x_first, a)
-            load(blocks[0], a)
-        for piece, units, held, splits in steps:
+            if a + 1 < PASSES:
+                load_w(0, a + 1)
+            load_x(a)
+        for q in range(1, BLOCKS):
             for a in range(PASSES):
-                load(piece, a)
-                if a == 1 and piece == blocks[1]:
+                load_w(q, a)
+                if q == 1 and a == 0:
                     nc.sync.dma_start(out=weights[:, 0:HALF], in_=wgo[:, 0:HALF])
-                if a == 1 and piece[0:2] == ("x", HALF):
+                if q == 1 and a == 3:
                     nc.sync.dma_start(out=weights[:, HALF:S], in_=wgo[:, HALF:S])
         for i in range(WINDOWS):
-            (nc.vector if i < 6 else nc.gpsimd).memset(windows[i][:], 0.0)
+            (nc.vector if i < 4 else nc.gpsimd).memset(windows[i][:], 0.0)
 
-        vcopy, scopy = nc.vector.tensor_copy, nc.scalar.copy
         bt = psum_b.tile([P, P], F32, name="bt")
-        scopy(out=b_rows[0:BLOCKS, :], in_=b_load[:])
+        vcopy(out=b_rows[0:BLOCKS, :], in_=b_load[:])
         nc.tensor.transpose(bt[:], b_rows[:], ident[:])
-        scopy(out=b_cols[:], in_=bt[:, 0:BLOCKS])
-        for a in range(PASSES):
-            group(x_first, a, scopy, P, HALF)
-            group(x_first, a, vcopy, 0, P)
-            group(blocks[0], a, scopy, 0, P)
-            quantize(x_first, a, a + 1)
-            quantize(blocks[0], a, a + 1)
-            for unit in first_units + first_held:
-                multiply(unit, a)
-        for unit in first_units:
-            place_own(unit)
-        waiting = first_held
-        on_vector = []
-        for piece, units, held, splits in steps:
-            width = piece[2] - piece[1]
-            for a0, a1 in splits:
-                for a in range(a0, a1):
-                    group(piece, a, vcopy if (piece[0:2], a) in on_vector else scopy, 0, width)
-                quantize(piece, a0, a1)
-                for a in range(a0, a1):
-                    for unit in units + held:
+        vcopy(out=b_cols[:], in_=bt[:, 0:BLOCKS])
+        pairs = [ring.tile([P, 2 * P * PACK], BF16, align_bytes=64, name="pair") for h in range(2)]
+        anchors = [pair[:].bitcast(F32)[:, i * HALF : i * HALF + 1] for pair in pairs for i in range(2)][1:]
+        for anchor in anchors:
+            vcopy(out=anchor, in_=b_cols[:, 0:1])
+        first, second, late = (0, 0, P), (0, P, HALF), (0, HALF, S)
+
+        def prepare_first(a):
+            interleave(scopy, w_first[a][:], w_raw[0][a][:])
+            quantize_w(0, a, a + 1, w_first[a][:])
+
+        prepare_first(0)
+        for a in range(PASSES - 1):
+            prepare_first(a + 1)
+            low, high = x_grouped[a % 2], x_grouped[(a + 1) % 2]
+            interleave(scopy, high[:], x_raw[a][:, :, HALF:S])
+            interleave(vcopy, low[:], x_raw[a][:, :, 0:HALF])
+            quantize_x(a, 0, HALF, low[:])
+            multiply(first, a)
+            multiply(second, a)
+            quantize_x(a, HALF, S, high[:])
+            multiply(late, a)
+        a = PASSES - 1
+        quarters = [x_grouped[(a + i) % 2][:, i // 2 * P * PACK : (i // 2 + 1) * P * PACK] for i in range(4)]
+        for i in range(4):
+            interleave(scopy if i % 2 else vcopy, quarters[i], x_raw[a][:, :, i * P : (i + 1) * P])
+        for i in range(4):
+            quantize_x(a, i * P, (i + 1) * P, quarters[i])
+            if i != 2:
+                multiply((first, second, None, late)[i], a)
+        y_first = keep.tile([P, HALF], F32, name="y_first")
+        add_bias(first, y_first[:, 0:P], anchors[0], 0, P // 2)
+        add_bias(first, y_first[:, 0:P], anchors[1], P // 2, P)
+        place(first, y_first[:, 0:P])
+        add_bias(second, y_first[:, P:HALF], anchors[2], 0, P)
+        place(second, y_first[:, P:HALF])
+        waiting = late
+        for q in range(1, BLOCKS):
+            units = [(q, 0, HALF), (q, HALF, S)] if q < HALVED else [(q, 0, S)]
+            for h in range(2):
+                pair = pairs[h] if q == 1 else ring.tile([P, 2 * P * PACK], BF16, align_bytes=64, name="pair")
+                grouped = [pair[:, i * P * PACK : (i + 1) * P * PACK] for i in range(2)]
+                if q == 1 and h == 0:
+                    grouped[0] = quarters[0]
+                for i in range(2):
+                    interleave(scopy, grouped[i], w_raw[q][2 * h + i][:])
+                if (q == 1 and h == 0) or (q <= 1):
+                    for i in range(2):
+                        quantize_w(q, 2 * h + i, 2 * h + i + 1, grouped[i])
+                else:
+                    quantize_w(q, 2 * h, 2 * h + 2, pair[:])
+                for unit in units:
+                    for a in range(2 * h, 2 * h + 2):
                         multiply(unit, a)
-            last = raw[piece][2][:].rearrange("p j c -> p (j c)")
-            at = 0
-            for unit in waiting:
-                place(unit, last[:, at : at + unit[2] - unit[1]])
-                at = at + unit[2] - unit[1]
-            for unit in units:
+            width = waiting[2] - waiting[1]
+            y = w_raw[q][2][:].rearrange("p j c -> p (j c)")[:, 0:width]
+            add_bias(waiting, y, b_cols[:, q - 1 : q], 0, width)
+            place(waiting, y)
+            for unit in units[:-1]:
                 place_own(unit)
-            waiting = held
-        for unit in waiting:
-            place_own(unit)
+            waiting = units[-1]
+        place_own(waiting)

@@ -1,7 +1,6 @@
 from contextlib import ExitStack
 
 import concourse.mybir as mybir
-from concourse.masks import make_identity
 
 K, M, T, S = 2048, 1024, 1024, 512
 FLOPS = 2 * K * M * S
@@ -23,6 +22,9 @@ BLOCKS = M // P
 HALF = S // 2
 WINDOWS = 6
 HALVED = 4
+SPLIT = 320
+QUAD = 32
+GROUP = 16
 
 
 def interleave(copy, grouped, raw):
@@ -36,25 +38,22 @@ def tile_list_hscat_bias_kernel(tc, x, w, b, wgo, offs, out):
     nc = tc.nc
     with ExitStack() as ctx:
         keep = ctx.enter_context(tc.tile_pool(name="keep", bufs=1))
-        ring = ctx.enter_context(tc.tile_pool(name="ring", bufs=2))
-        psum = ctx.enter_context(tc.psum_pool(name="psum", bufs=7))
-        psum_b = ctx.enter_context(tc.psum_pool(name="psum_b", bufs=1))
+        psum = ctx.enter_context(tc.psum_pool(name="psum", bufs=8))
 
         offsets = keep.tile([P, S // 16], U16, name="offsets")
-        weights = keep.tile([P, S], F32, name="weights")
-        b_rows = keep.tile([P, P], F32, name="b_rows")
-        b_load = keep.tile([BLOCKS, P], F32, name="b_load")
-        ident = keep.tile([P, P], F32, name="ident")
-        b_cols = keep.tile([P, BLOCKS], F32, name="b_cols")
+        weights = keep.tile([P, S], F32, align_bytes=64, name="weights")
+        rows_in = keep.tile([P, S + BLOCKS * QUAD], F32, align_bytes=64, name="rows_in")
+        turned = keep.tile([P, S + BLOCKS * QUAD], F32, align_bytes=64, name="turned")
+        spread = keep.tile([P, S], F32, align_bytes=64, name="spread")
         windows = [keep.tile([P, T], F32, name=f"window{i}") for i in range(WINDOWS)]
         x_codes = keep.tile([P, PASSES, S], U32, align_bytes=64, name="x_codes")
         x_scales = keep.tile([P, PASSES, S], U8, align_bytes=64, name="x_scales")
         w_codes = [keep.tile([P, PASSES, P], U32, align_bytes=64, name=f"w_codes{q}") for q in range(BLOCKS)]
         w_scales = [keep.tile([P, PASSES, P], U8, align_bytes=64, name=f"w_scales{q}") for q in range(BLOCKS)]
-        x_raw = [keep.tile([P, PACK, S], F32, name=f"x_raw{a}") for a in range(PASSES)]
-        w_raw = [[keep.tile([P, PACK, P], F32, name=f"w_raw{q}_{a}") for a in range(PASSES)] for q in range(BLOCKS)]
-        x_grouped = [keep.tile([P, HALF * PACK], BF16, align_bytes=64, name=f"x_grouped{i}") for i in range(2)]
-        w_first = [keep.tile([P, P * PACK], BF16, align_bytes=64, name=f"w_first{a}") for a in range(PASSES)]
+        x_raw = [keep.tile([P, PACK, S], F32, align_bytes=64, name=f"x_raw{a}") for a in range(PASSES)]
+        w_raw = [[keep.tile([P, PACK, P], F32, align_bytes=64, name=f"w_raw{q}_{a}") for a in range(PASSES)] for q in range(BLOCKS)]
+        x_grouped = keep.tile([P, S * PACK], BF16, align_bytes=64, name="x_grouped")
+        w_first = [keep.tile([P, P * PACK], BF16, align_bytes=64, name=f"w_first{a}") for a in range(PASSES - 1)]
         vcopy, scopy = nc.vector.tensor_copy, nc.scalar.copy
 
         def load_x(a):
@@ -93,8 +92,8 @@ def tile_list_hscat_bias_kernel(tc, x, w, b, wgo, offs, out):
                 stop=(a == PASSES - 1),
             )
 
-        def add_bias(unit, y, bias, i0, i1):
-            nc.scalar.activation(out=y[:, i0:i1], in_=accs[unit][:, i0:i1], func=IDENTITY, bias=bias)
+        def bias_of(q):
+            return turned[:, S + q * QUAD : S + q * QUAD + 1]
 
         def place(unit, y):
             q, c0, c1 = unit
@@ -107,92 +106,98 @@ def tile_list_hscat_bias_kernel(tc, x, w, b, wgo, offs, out):
             if c1 == S:
                 nc.sync.dma_start(out=out[q * P : (q + 1) * P, :], in_=windows[q % WINDOWS][:])
 
+        def place_on(unit, room):
+            q, c0, c1 = unit
+            y = room[:, 0 : c1 - c0]
+            nc.scalar.activation(out=y, in_=accs[unit][:, 0 : c1 - c0], func=IDENTITY, bias=bias_of(q))
+            place(unit, y)
+
         def place_own(unit):
             q, c0, c1 = unit
-            own = keep.tile([P, c1 - c0], F32, name=f"y{q}_{c0}")
-            add_bias(unit, own[:], b_cols[:, q : q + 1], 0, c1 - c0)
-            place(unit, own[:])
+            place_on(unit, keep.tile([P, c1 - c0], F32, name=f"y{q}_{c0}"))
 
-        nc.gpsimd.memset(b_rows[:], 0.0)
-        make_identity(nc, ident[:])
-        nc.sync.dma_start(out=b_load[:], in_=b.rearrange("(c p) -> c p", p=P))
-        nc.sync.dma_start(offsets[:], offs)
+        nc.gpsimd.memset(rows_in[:], 0.0)
         load_w(0, 0)
+        nc.sync.dma_start(
+            out=rows_in[0:P:QUAD, S:].rearrange("u (q i) -> u q i", i=QUAD),
+            in_=b.rearrange("(q u i) -> u q i", u=P // QUAD, i=QUAD),
+        )
+        nc.sync.dma_start(out=rows_in[0:P:GROUP, 0:S], in_=wgo[0:P:GROUP, :])
         for a in range(PASSES):
-            if a + 1 < PASSES:
+            if a + 1 < PASSES - 1:
                 load_w(0, a + 1)
             load_x(a)
+        load_w(0, PASSES - 1)
+        nc.sync.dma_start(offsets[:], offs)
         for q in range(1, BLOCKS):
             for a in range(PASSES):
                 load_w(q, a)
-                if q == 1 and a == 0:
-                    nc.sync.dma_start(out=weights[:, 0:HALF], in_=wgo[:, 0:HALF])
-                if q == 1 and a == 3:
-                    nc.sync.dma_start(out=weights[:, HALF:S], in_=wgo[:, HALF:S])
         for i in range(WINDOWS):
             (nc.vector if i < 4 else nc.gpsimd).memset(windows[i][:], 0.0)
 
-        bt = psum_b.tile([P, P], F32, name="bt")
-        vcopy(out=b_rows[0:BLOCKS, :], in_=b_load[:])
-        nc.tensor.transpose(bt[:], b_rows[:], ident[:])
-        vcopy(out=b_cols[:], in_=bt[:, 0:BLOCKS])
-        pairs = [ring.tile([P, 2 * P * PACK], BF16, align_bytes=64, name="pair") for h in range(2)]
-        anchors = [pair[:].bitcast(F32)[:, i * HALF : i * HALF + 1] for pair in pairs for i in range(2)][1:]
-        for anchor in anchors:
-            vcopy(out=anchor, in_=b_cols[:, 0:1])
+        nc.vector.transpose(turned[:], rows_in[:])
+        heads = turned[:, 0:S].rearrange("p (g r) -> p g r", r=GROUP)[:, :, 0:1]
+        vcopy(out=spread[:].rearrange("p (g r) -> p g r", r=GROUP), in_=heads.to_broadcast([P, S // GROUP, GROUP]))
+        nc.vector.transpose(weights[:], spread[:])
         first, second, late = (0, 0, P), (0, P, HALF), (0, HALF, S)
 
         def prepare_first(a):
             interleave(scopy, w_first[a][:], w_raw[0][a][:])
             quantize_w(0, a, a + 1, w_first[a][:])
 
-        prepare_first(0)
+        def columns(grouped, c0, c1):
+            return grouped[:, c0 * PACK : c1 * PACK]
+
         for a in range(PASSES - 1):
-            prepare_first(a + 1)
-            low, high = x_grouped[a % 2], x_grouped[(a + 1) % 2]
-            interleave(scopy, high[:], x_raw[a][:, :, HALF:S])
-            interleave(vcopy, low[:], x_raw[a][:, :, 0:HALF])
-            quantize_x(a, 0, HALF, low[:])
-            multiply(first, a)
-            multiply(second, a)
-            quantize_x(a, HALF, S, high[:])
-            multiply(late, a)
+            prepare_first(a)
+            interleave(scopy, columns(x_grouped, SPLIT, S), x_raw[a][:, :, SPLIT:S])
+            interleave(vcopy, columns(x_grouped, 0, SPLIT), x_raw[a][:, :, 0:SPLIT])
+            quantize_x(a, 0, S, x_grouped[:])
+            for unit in (first, second, late):
+                multiply(unit, a)
         a = PASSES - 1
-        quarters = [x_grouped[(a + i) % 2][:, i // 2 * P * PACK : (i // 2 + 1) * P * PACK] for i in range(4)]
-        for i in range(4):
-            interleave(scopy if i % 2 else vcopy, quarters[i], x_raw[a][:, :, i * P : (i + 1) * P])
-        for i in range(4):
-            quantize_x(a, i * P, (i + 1) * P, quarters[i])
-            if i != 2:
-                multiply((first, second, None, late)[i], a)
-        y_first = keep.tile([P, HALF], F32, name="y_first")
-        add_bias(first, y_first[:, 0:P], anchors[0], 0, P // 2)
-        add_bias(first, y_first[:, 0:P], anchors[1], P // 2, P)
-        place(first, y_first[:, 0:P])
-        add_bias(second, y_first[:, P:HALF], anchors[2], 0, P)
-        place(second, y_first[:, P:HALF])
+        spent = x_raw[a - 1][:].rearrange("p j c -> p (j c)").bitcast(BF16)
+        low, high = columns(x_grouped, 0, HALF), columns(spent, 0, HALF)
+        w_last, w_next = columns(x_grouped, HALF, HALF + P), columns(x_grouped, HALF + P, S)
+        interleave(scopy, high, x_raw[a][:, :, HALF:S])
+        interleave(vcopy, low, x_raw[a][:, :, 0:HALF])
+        interleave(vcopy, w_last, w_raw[0][a][:])
+        quantize_x(a, 0, HALF, low)
+        quantize_w(0, a, a + 1, w_last)
+        multiply(first, a)
+        multiply(second, a)
+        quantize_x(a, HALF, S, high)
+        multiply(late, a)
+        units = [(1, 0, HALF), (1, HALF, S)]
+        spare = [w_raw[1][h][:].rearrange("p j c -> p (j c)").bitcast(BF16) for h in range(2)]
+
+        def prepare_second(copy, a0, a1, grouped):
+            for a in range(a0, a1):
+                interleave(copy, columns(grouped, (a - a0) * P, (a - a0 + 1) * P), w_raw[1][a][:])
+            quantize_w(1, a0, a1, grouped)
+            for unit in units:
+                for a in range(a0, a1):
+                    multiply(unit, a)
+
+        prepare_second(vcopy, 0, 1, w_next)
+        place_own(first)
+        place_own(second)
+        prepare_second(scopy, 1, 2, columns(spare[0], 0, P))
+        prepare_second(scopy, 2, 3, columns(spare[0], P, HALF))
+        prepare_second(scopy, 3, 4, columns(spare[1], P, HALF))
         waiting = late
         for q in range(1, BLOCKS):
-            units = [(q, 0, HALF), (q, HALF, S)] if q < HALVED else [(q, 0, S)]
-            for h in range(2):
-                pair = pairs[h] if q == 1 else ring.tile([P, 2 * P * PACK], BF16, align_bytes=64, name="pair")
-                grouped = [pair[:, i * P * PACK : (i + 1) * P * PACK] for i in range(2)]
-                if q == 1 and h == 0:
-                    grouped[0] = quarters[0]
-                for i in range(2):
-                    interleave(scopy, grouped[i], w_raw[q][2 * h + i][:])
-                if (q == 1 and h == 0) or (q <= 1):
+            if q > 1:
+                units = [(q, 0, HALF), (q, HALF, S)] if q < HALVED else [(q, 0, S)]
+                for h in range(2):
+                    pair = spare[h]
                     for i in range(2):
-                        quantize_w(q, 2 * h + i, 2 * h + i + 1, grouped[i])
-                else:
-                    quantize_w(q, 2 * h, 2 * h + 2, pair[:])
-                for unit in units:
-                    for a in range(2 * h, 2 * h + 2):
-                        multiply(unit, a)
-            width = waiting[2] - waiting[1]
-            y = w_raw[q][2][:].rearrange("p j c -> p (j c)")[:, 0:width]
-            add_bias(waiting, y, b_cols[:, q - 1 : q], 0, width)
-            place(waiting, y)
+                        interleave(scopy, columns(pair, i * P, (i + 1) * P), w_raw[q][2 * h + i][:])
+                    quantize_w(q, 2 * h, 2 * h + 2, pair)
+                    for unit in units:
+                        for a in range(2 * h, 2 * h + 2):
+                            multiply(unit, a)
+            place_on(waiting, w_raw[q][2][:].rearrange("p j c -> p (j c)"))
             for unit in units[:-1]:
                 place_own(unit)
             waiting = units[-1]

@@ -21,7 +21,7 @@ PASSES = K // K_PASS
 BLOCKS = M // P
 HALF = S // 2
 WINDOWS = 6
-HALVED = 4
+HALVED = 2
 SPLIT = 320
 QUAD = 32
 GROUP = 16
@@ -51,7 +51,11 @@ def tile_list_hscat_bias_kernel(tc, x, w, b, wgo, offs, out):
         w_codes = [keep.tile([P, PASSES, P], U32, align_bytes=64, name=f"w_codes{q}") for q in range(BLOCKS)]
         w_scales = [keep.tile([P, PASSES, P], U8, align_bytes=64, name=f"w_scales{q}") for q in range(BLOCKS)]
         x_raw = [keep.tile([P, PACK, S], F32, align_bytes=64, name=f"x_raw{a}") for a in range(PASSES)]
-        w_raw = [[keep.tile([P, PACK, P], F32, align_bytes=64, name=f"w_raw{q}_{a}") for a in range(PASSES)] for q in range(BLOCKS)]
+        w_rows = [keep.tile([P, PASSES * PACK * P], F32, align_bytes=64, name=f"w_rows{q}") for q in range(BLOCKS)]
+        w_raw = [
+            [rows[:, a * PACK * P : (a + 1) * PACK * P].rearrange("p (j c) -> p j c", j=PACK) for a in range(PASSES)]
+            for rows in w_rows
+        ]
         x_grouped = keep.tile([P, S * PACK], BF16, align_bytes=64, name="x_grouped")
         w_first = [keep.tile([P, P * PACK], BF16, align_bytes=64, name=f"w_first{a}") for a in range(PASSES - 1)]
         vcopy, scopy = nc.vector.tensor_copy, nc.scalar.copy
@@ -62,7 +66,7 @@ def tile_list_hscat_bias_kernel(tc, x, w, b, wgo, offs, out):
 
         def load_w(q, a):
             rows = w[a * K_PASS : (a + 1) * K_PASS, q * P : (q + 1) * P]
-            nc.sync.dma_start(out=w_raw[q][a][:], in_=rows.rearrange("(p j) c -> p j c", j=PACK))
+            nc.sync.dma_start(out=w_raw[q][a], in_=rows.rearrange("(p j) c -> p j c", j=PACK))
 
         def quantize_x(a, c0, c1, grouped):
             nc.vector.quantize_mx(
@@ -139,10 +143,10 @@ def tile_list_hscat_bias_kernel(tc, x, w, b, wgo, offs, out):
         heads = turned[:, 0:S].rearrange("p (g r) -> p g r", r=GROUP)[:, :, 0:1]
         vcopy(out=spread[:].rearrange("p (g r) -> p g r", r=GROUP), in_=heads.to_broadcast([P, S // GROUP, GROUP]))
         nc.vector.transpose(weights[:], spread[:])
-        first, second, late = (0, 0, P), (0, P, HALF), (0, HALF, S)
+        first, late = (0, 0, HALF), (0, HALF, S)
 
         def prepare_first(a):
-            interleave(scopy, w_first[a][:], w_raw[0][a][:])
+            interleave(scopy, w_first[a][:], w_raw[0][a])
             quantize_w(0, a, a + 1, w_first[a][:])
 
         def columns(grouped, c0, c1):
@@ -153,7 +157,7 @@ def tile_list_hscat_bias_kernel(tc, x, w, b, wgo, offs, out):
             interleave(scopy, columns(x_grouped, SPLIT, S), x_raw[a][:, :, SPLIT:S])
             interleave(vcopy, columns(x_grouped, 0, SPLIT), x_raw[a][:, :, 0:SPLIT])
             quantize_x(a, 0, S, x_grouped[:])
-            for unit in (first, second, late):
+            for unit in (first, late):
                 multiply(unit, a)
         a = PASSES - 1
         spent = x_raw[a - 1][:].rearrange("p j c -> p (j c)").bitcast(BF16)
@@ -161,19 +165,18 @@ def tile_list_hscat_bias_kernel(tc, x, w, b, wgo, offs, out):
         w_last, w_next = columns(x_grouped, HALF, HALF + P), columns(x_grouped, HALF + P, S)
         interleave(scopy, high, x_raw[a][:, :, HALF:S])
         interleave(vcopy, low, x_raw[a][:, :, 0:HALF])
-        interleave(vcopy, w_last, w_raw[0][a][:])
+        interleave(vcopy, w_last, w_raw[0][a])
         quantize_x(a, 0, HALF, low)
         quantize_w(0, a, a + 1, w_last)
         multiply(first, a)
-        multiply(second, a)
         quantize_x(a, HALF, S, high)
         multiply(late, a)
         units = [(1, 0, HALF), (1, HALF, S)]
-        spare = [w_raw[1][h][:].rearrange("p j c -> p (j c)").bitcast(BF16) for h in range(2)]
+        spare = w_rows[1][:, 0 : 2 * PACK * P].bitcast(BF16)
 
         def prepare_second(copy, a0, a1, grouped):
             for a in range(a0, a1):
-                interleave(copy, columns(grouped, (a - a0) * P, (a - a0 + 1) * P), w_raw[1][a][:])
+                interleave(copy, columns(grouped, (a - a0) * P, (a - a0 + 1) * P), w_raw[1][a])
             quantize_w(1, a0, a1, grouped)
             for unit in units:
                 for a in range(a0, a1):
@@ -181,23 +184,22 @@ def tile_list_hscat_bias_kernel(tc, x, w, b, wgo, offs, out):
 
         prepare_second(vcopy, 0, 1, w_next)
         place_own(first)
-        place_own(second)
-        prepare_second(scopy, 1, 2, columns(spare[0], 0, P))
-        prepare_second(scopy, 2, 3, columns(spare[0], P, HALF))
-        prepare_second(scopy, 3, 4, columns(spare[1], P, HALF))
+        prepare_second(scopy, 1, 2, columns(spare, 0, P))
+        prepare_second(scopy, 2, 3, columns(spare, P, HALF))
+        prepare_second(scopy, 3, 4, columns(spare, HALF + P, S))
         waiting = late
         for q in range(1, BLOCKS):
             if q > 1:
                 units = [(q, 0, HALF), (q, HALF, S)] if q < HALVED else [(q, 0, S)]
-                for h in range(2):
-                    pair = spare[h]
-                    for i in range(2):
-                        interleave(scopy, columns(pair, i * P, (i + 1) * P), w_raw[q][2 * h + i][:])
-                    quantize_w(q, 2 * h, 2 * h + 2, pair)
+                step = PASSES if HALVED < q < BLOCKS - 1 else 2
+                for a0 in range(0, PASSES, step):
+                    for a in range(a0, a0 + step):
+                        interleave(scopy, columns(spare, a * P, (a + 1) * P), w_raw[q][a])
+                    quantize_w(q, a0, a0 + step, columns(spare, a0 * P, (a0 + step) * P))
                     for unit in units:
-                        for a in range(2 * h, 2 * h + 2):
+                        for a in range(a0, a0 + step):
                             multiply(unit, a)
-            place_on(waiting, w_raw[q][2][:].rearrange("p j c -> p (j c)"))
+            place_on(waiting, w_rows[q][:, 2 * PACK * P : 3 * PACK * P])
             for unit in units[:-1]:
                 place_own(unit)
             waiting = units[-1]

@@ -21,7 +21,7 @@ PASSES = K // K_PASS
 BLOCKS = M // P
 HALF = S // 2
 WINDOWS = 6
-HALVED = 2
+HALVED = 3
 SPLIT = 320
 QUAD = 32
 GROUP = 16
@@ -137,11 +137,11 @@ def tile_list_hscat_bias_kernel(tc, x, w, b, wgo, offs, out):
             for a in range(PASSES):
                 load_w(q, a)
         for i in range(WINDOWS):
-            (nc.vector if i < 4 else nc.gpsimd).memset(windows[i][:], 0.0)
+            (nc.vector if i < 3 else nc.gpsimd).memset(windows[i][:], 0.0)
 
         nc.vector.transpose(turned[:], rows_in[:])
         heads = turned[:, 0:S].rearrange("p (g r) -> p g r", r=GROUP)[:, :, 0:1]
-        vcopy(out=spread[:].rearrange("p (g r) -> p g r", r=GROUP), in_=heads.to_broadcast([P, S // GROUP, GROUP]))
+        scopy(out=spread[:].rearrange("p (g r) -> p g r", r=GROUP), in_=heads.to_broadcast([P, S // GROUP, GROUP]))
         nc.vector.transpose(weights[:], spread[:])
         first, late = (0, 0, HALF), (0, HALF, S)
 

@@ -137,11 +137,12 @@ def tile_list_hscat_bias_kernel(tc, x, w, b, wgo, offs, out):
             for a in range(PASSES):
                 load_w(q, a)
         for i in range(WINDOWS):
-            (nc.vector if i < 3 else nc.gpsimd).memset(windows[i][:], 0.0)
+            nc.vector.memset(windows[i][:], 0.0)
 
-        nc.vector.transpose(turned[:], rows_in[:])
+        nc.vector.transpose(turned[:, 0:S], rows_in[:, 0:S])
+        nc.vector.transpose(turned[:, S:], rows_in[:, S:])
         heads = turned[:, 0:S].rearrange("p (g r) -> p g r", r=GROUP)[:, :, 0:1]
-        scopy(out=spread[:].rearrange("p (g r) -> p g r", r=GROUP), in_=heads.to_broadcast([P, S // GROUP, GROUP]))
+        vcopy(out=spread[:].rearrange("p (g r) -> p g r", r=GROUP), in_=heads.to_broadcast([P, S // GROUP, GROUP]))
         nc.vector.transpose(weights[:], spread[:])
         first, late = (0, 0, HALF), (0, HALF, S)
 

@@ -25,6 +25,7 @@ HALVED = 3
 SPLIT = 320
 QUAD = 32
 GROUP = 16
+BIAS_ROW = 4
 
 
 def interleave(copy, grouped, raw):
@@ -42,8 +43,8 @@ def tile_list_hscat_bias_kernel(tc, x, w, b, wgo, offs, out):
 
         offsets = keep.tile([P, S // 16], U16, name="offsets")
         weights = keep.tile([P, S], F32, align_bytes=64, name="weights")
-        rows_in = keep.tile([P, S + BLOCKS * QUAD], F32, align_bytes=64, name="rows_in")
-        turned = keep.tile([P, S + BLOCKS * QUAD], F32, align_bytes=64, name="turned")
+        rows_in = keep.tile([P, HALF], F32, align_bytes=64, name="rows_in")
+        turned = keep.tile([P, HALF], F32, align_bytes=64, name="turned")
         spread = keep.tile([P, S], F32, align_bytes=64, name="spread")
         windows = [keep.tile([P, T], F32, name=f"window{i}") for i in range(WINDOWS)]
         x_codes = keep.tile([P, PASSES, S], U32, align_bytes=64, name="x_codes")
@@ -97,7 +98,7 @@ def tile_list_hscat_bias_kernel(tc, x, w, b, wgo, offs, out):
             )
 
         def bias_of(q):
-            return turned[:, S + q * QUAD : S + q * QUAD + 1]
+            return turned[:, q * QUAD + BIAS_ROW : q * QUAD + BIAS_ROW + 1]
 
         def place(unit, y):
             q, c0, c1 = unit
@@ -120,13 +121,14 @@ def tile_list_hscat_bias_kernel(tc, x, w, b, wgo, offs, out):
             q, c0, c1 = unit
             place_on(unit, keep.tile([P, c1 - c0], F32, name=f"y{q}_{c0}"))
 
-        nc.gpsimd.memset(rows_in[:], 0.0)
+        nc.vector.memset(rows_in[:], 0.0)
         load_w(0, 0)
         nc.sync.dma_start(
-            out=rows_in[0:P:QUAD, S:].rearrange("u (q i) -> u q i", i=QUAD),
+            out=rows_in[BIAS_ROW:P:QUAD, :].rearrange("u (q i) -> u q i", i=QUAD),
             in_=b.rearrange("(q u i) -> u q i", u=P // QUAD, i=QUAD),
         )
-        nc.sync.dma_start(out=rows_in[0:P:GROUP, 0:S], in_=wgo[0:P:GROUP, :])
+        half_rows = wgo.rearrange("p (v e) -> (p v) e", e=HALF)
+        nc.sync.dma_start(out=rows_in[0 : P : GROUP // 2, :], in_=half_rows[0 : 2 * P : GROUP + 1, :])
         for a in range(PASSES):
             if a + 1 < PASSES - 1:
                 load_w(0, a + 1)
@@ -139,10 +141,12 @@ def tile_list_hscat_bias_kernel(tc, x, w, b, wgo, offs, out):
         for i in range(WINDOWS):
             nc.vector.memset(windows[i][:], 0.0)
 
-        nc.vector.transpose(turned[:, 0:S], rows_in[:, 0:S])
-        nc.vector.transpose(turned[:, S:], rows_in[:, S:])
-        heads = turned[:, 0:S].rearrange("p (g r) -> p g r", r=GROUP)[:, :, 0:1]
-        vcopy(out=spread[:].rearrange("p (g r) -> p g r", r=GROUP), in_=heads.to_broadcast([P, S // GROUP, GROUP]))
+        nc.vector.transpose(turned[:], rows_in[:])
+        heads = turned[:].rearrange("p (g v r) -> p v g r", v=2, r=GROUP // 2)[:, :, :, 0:1]
+        vcopy(
+            out=spread[:].rearrange("p (v g r) -> p v g r", v=2, r=GROUP),
+            in_=heads.to_broadcast([P, 2, HALF // GROUP, GROUP]),
+        )
         nc.vector.transpose(weights[:], spread[:])
         first, late = (0, 0, HALF), (0, HALF, S)
 

@@ -23,6 +23,7 @@ HALF = S // 2
 WINDOWS = 6
 HALVED = 3
 SPLIT = 320
+EARLY = 192
 QUAD = 32
 GROUP = 16
 BIAS_ROW = 4
@@ -111,11 +112,13 @@ def tile_list_hscat_bias_kernel(tc, x, w, b, wgo, offs, out):
             if c1 == S:
                 nc.sync.dma_start(out=out[q * P : (q + 1) * P, :], in_=windows[q % WINDOWS][:])
 
+        def add_bias(unit, y, i0, i1):
+            nc.scalar.activation(out=y, in_=accs[unit][:, i0:i1], func=IDENTITY, bias=bias_of(unit[0]))
+
         def place_on(unit, room):
             q, c0, c1 = unit
-            y = room[:, 0 : c1 - c0]
-            nc.scalar.activation(out=y, in_=accs[unit][:, 0 : c1 - c0], func=IDENTITY, bias=bias_of(q))
-            place(unit, y)
+            add_bias(unit, room[:, 0 : c1 - c0], 0, c1 - c0)
+            place(unit, room[:, 0 : c1 - c0])
 
         def place_own(unit):
             q, c0, c1 = unit
@@ -148,7 +151,7 @@ def tile_list_hscat_bias_kernel(tc, x, w, b, wgo, offs, out):
             in_=heads.to_broadcast([P, 2, HALF // GROUP, GROUP]),
         )
         nc.vector.transpose(weights[:], spread[:])
-        first, late = (0, 0, HALF), (0, HALF, S)
+        first, second, late = (0, 0, P), (0, P, HALF), (0, HALF, S)
 
         def prepare_first(a):
             interleave(scopy, w_first[a][:], w_raw[0][a])
@@ -162,7 +165,7 @@ def tile_list_hscat_bias_kernel(tc, x, w, b, wgo, offs, out):
             interleave(scopy, columns(x_grouped, SPLIT, S), x_raw[a][:, :, SPLIT:S])
             interleave(vcopy, columns(x_grouped, 0, SPLIT), x_raw[a][:, :, 0:SPLIT])
             quantize_x(a, 0, S, x_grouped[:])
-            for unit in (first, late):
+            for unit in (first, second, late):
                 multiply(unit, a)
         a = PASSES - 1
         spent = x_raw[a - 1][:].rearrange("p j c -> p (j c)").bitcast(BF16)
@@ -174,6 +177,7 @@ def tile_list_hscat_bias_kernel(tc, x, w, b, wgo, offs, out):
         quantize_x(a, 0, HALF, low)
         quantize_w(0, a, a + 1, w_last)
         multiply(first, a)
+        multiply(second, a)
         quantize_x(a, HALF, S, high)
         multiply(late, a)
         units = [(1, 0, HALF), (1, HALF, S)]
@@ -188,11 +192,17 @@ def tile_list_hscat_bias_kernel(tc, x, w, b, wgo, offs, out):
                     multiply(unit, a)
 
         prepare_second(vcopy, 0, 1, w_next)
-        place_own(first)
+        y_first = keep.tile([P, HALF], F32, name="y_first")
+        add_bias(first, y_first[:, 0:P], 0, P)
+        add_bias(second, y_first[:, P:HALF], 0, P)
+        place((0, 0, HALF), y_first[:])
         prepare_second(scopy, 1, 2, columns(spare, 0, P))
         prepare_second(scopy, 2, 3, columns(spare, P, HALF))
-        prepare_second(scopy, 3, 4, columns(spare, HALF + P, S))
-        waiting = late
+        y_late = w_rows[1][:, 2 * PACK * P - EARLY : 2 * PACK * P - EARLY + HALF]
+        add_bias(late, y_late[:, 0:EARLY], 0, EARLY)
+        prepare_second(scopy, 3, 4, columns(spare, HALF, HALF + P))
+        add_bias(late, y_late[:, EARLY:HALF], EARLY, HALF)
+        place(late, y_late)
         for q in range(1, BLOCKS):
             if q > 1:
                 units = [(q, 0, HALF), (q, HALF, S)] if q < HALVED else [(q, 0, S)]
@@ -204,7 +214,7 @@ def tile_list_hscat_bias_kernel(tc, x, w, b, wgo, offs, out):
                     for unit in units:
                         for a in range(a0, a0 + step):
                             multiply(unit, a)
-            place_on(waiting, w_rows[q][:, 2 * PACK * P : 3 * PACK * P])
+                place_on(waiting, w_rows[q][:, 2 * PACK * P : 3 * PACK * P])
             for unit in units[:-1]:
                 place_own(unit)
             waiting = units[-1]

@@ -22,7 +22,7 @@ BLOCKS = M // P
 HALF = S // 2
 WINDOWS = 6
 HALVED = 3
-SPLIT = 320
+SPLIT = 256
 EARLY = 192
 QUAD = 32
 GROUP = 16
@@ -58,7 +58,7 @@ def tile_list_hscat_bias_kernel(tc, x, w, b, wgo, offs, out):
             [rows[:, a * PACK * P : (a + 1) * PACK * P].rearrange("p (j c) -> p j c", j=PACK) for a in range(PASSES)]
             for rows in w_rows
         ]
-        x_grouped = keep.tile([P, S * PACK], BF16, align_bytes=64, name="x_grouped")
+        x_grouped = [keep.tile([P, S * PACK], BF16, align_bytes=64, name=f"x_grouped{a}") for a in range(PASSES - 1)]
         w_first = [keep.tile([P, P * PACK], BF16, align_bytes=64, name=f"w_first{a}") for a in range(PASSES - 1)]
         vcopy, scopy = nc.vector.tensor_copy, nc.scalar.copy
 
@@ -68,7 +68,8 @@ def tile_list_hscat_bias_kernel(tc, x, w, b, wgo, offs, out):
 
         def load_w(q, a):
             rows = w[a * K_PASS : (a + 1) * K_PASS, q * P : (q + 1) * P]
-            nc.sync.dma_start(out=w_raw[q][a], in_=rows.rearrange("(p j) c -> p j c", j=PACK))
+            queue = nc.scalar if q == 0 and a < PASSES - 1 else nc.sync
+            queue.dma_start(out=w_raw[q][a], in_=rows.rearrange("(p j) c -> p j c", j=PACK))
 
         def quantize_x(a, c0, c1, grouped):
             nc.vector.quantize_mx(
@@ -125,16 +126,16 @@ def tile_list_hscat_bias_kernel(tc, x, w, b, wgo, offs, out):
             place_on(unit, keep.tile([P, c1 - c0], F32, name=f"y{q}_{c0}"))
 
         nc.vector.memset(rows_in[:], 0.0)
-        load_w(0, 0)
+        for a in range(PASSES - 1):
+            load_w(0, a)
+        load_x(0)
         nc.sync.dma_start(
             out=rows_in[BIAS_ROW:P:QUAD, :].rearrange("u (q i) -> u q i", i=QUAD),
             in_=b.rearrange("(q u i) -> u q i", u=P // QUAD, i=QUAD),
         )
         half_rows = wgo.rearrange("p (v e) -> (p v) e", e=HALF)
         nc.sync.dma_start(out=rows_in[0 : P : GROUP // 2, :], in_=half_rows[0 : 2 * P : GROUP + 1, :])
-        for a in range(PASSES):
-            if a + 1 < PASSES - 1:
-                load_w(0, a + 1)
+        for a in range(1, PASSES):
             load_x(a)
         load_w(0, PASSES - 1)
         nc.sync.dma_start(offsets[:], offs)
@@ -162,15 +163,15 @@ def tile_list_hscat_bias_kernel(tc, x, w, b, wgo, offs, out):
 
         for a in range(PASSES - 1):
             prepare_first(a)
-            interleave(scopy, columns(x_grouped, SPLIT, S), x_raw[a][:, :, SPLIT:S])
-            interleave(vcopy, columns(x_grouped, 0, SPLIT), x_raw[a][:, :, 0:SPLIT])
-            quantize_x(a, 0, S, x_grouped[:])
+            interleave(scopy, columns(x_grouped[a], SPLIT, S), x_raw[a][:, :, SPLIT:S])
+            interleave(vcopy, columns(x_grouped[a], 0, SPLIT), x_raw[a][:, :, 0:SPLIT])
+            quantize_x(a, 0, S, x_grouped[a][:])
             for unit in (first, second, late):
                 multiply(unit, a)
         a = PASSES - 1
         spent = x_raw[a - 1][:].rearrange("p j c -> p (j c)").bitcast(BF16)
-        low, high = columns(x_grouped, 0, HALF), columns(spent, 0, HALF)
-        w_last, w_next = columns(x_grouped, HALF, HALF + P), columns(x_grouped, HALF + P, S)
+        low, high = columns(x_grouped[a - 1], 0, HALF), columns(spent, 0, HALF)
+        w_last, w_next = columns(x_grouped[a - 1], HALF, HALF + P), columns(x_grouped[a - 1], HALF + P, S)
         interleave(scopy, high, x_raw[a][:, :, HALF:S])
         interleave(vcopy, low, x_raw[a][:, :, 0:HALF])
         interleave(vcopy, w_last, w_raw[0][a])

@@ -27,6 +27,7 @@ EARLY = 192
 QUAD = 32
 GROUP = 16
 BIAS_ROW = 4
+SHARE = 64
 
 
 def interleave(copy, grouped, raw):
@@ -53,11 +54,16 @@ def tile_list_hscat_bias_kernel(tc, x, w, b, wgo, offs, out):
         w_codes = [keep.tile([P, PASSES, P], U32, align_bytes=64, name=f"w_codes{q}") for q in range(BLOCKS)]
         w_scales = [keep.tile([P, PASSES, P], U8, align_bytes=64, name=f"w_scales{q}") for q in range(BLOCKS)]
         x_raw = [keep.tile([P, PACK, S], F32, align_bytes=64, name=f"x_raw{a}") for a in range(PASSES)]
-        w_rows = [keep.tile([P, PASSES * PACK * P], F32, align_bytes=64, name=f"w_rows{q}") for q in range(BLOCKS)]
-        w_raw = [
-            [rows[:, a * PACK * P : (a + 1) * PACK * P].rearrange("p (j c) -> p j c", j=PACK) for a in range(PASSES)]
-            for rows in w_rows
+        gaps = [EARLY if q == 1 else 0 for q in range(BLOCKS)]
+        w_rows = [
+            keep.tile([P, PASSES * PACK * P + gaps[q]], F32, align_bytes=64, name=f"w_rows{q}") for q in range(BLOCKS)
         ]
+        starts = [[a * PACK * P + (gaps[q] if a >= 2 else 0) for a in range(PASSES)] for q in range(BLOCKS)]
+        w_raw = [
+            [w_rows[q][:, i : i + PACK * P].rearrange("p (j c) -> p j c", j=PACK) for i in starts[q]]
+            for q in range(BLOCKS)
+        ]
+        w_second = keep.tile([P, (P + SHARE) * PACK], BF16, align_bytes=64, name="w_second")
         x_grouped = [keep.tile([P, S * PACK], BF16, align_bytes=64, name=f"x_grouped{a}") for a in range(PASSES - 1)]
         w_first = [keep.tile([P, P * PACK], BF16, align_bytes=64, name=f"w_first{a}") for a in range(PASSES - 1)]
         vcopy, scopy = nc.vector.tensor_copy, nc.scalar.copy
@@ -138,9 +144,10 @@ def tile_list_hscat_bias_kernel(tc, x, w, b, wgo, offs, out):
         for a in range(1, PASSES):
             load_x(a)
         load_w(0, PASSES - 1)
-        nc.sync.dma_start(offsets[:], offs)
         for q in range(1, BLOCKS):
             for a in range(PASSES):
+                if (q, a) == (1, 2):
+                    nc.sync.dma_start(offsets[:], offs)
                 load_w(q, a)
         for i in range(WINDOWS):
             nc.vector.memset(windows[i][:], 0.0)
@@ -171,7 +178,7 @@ def tile_list_hscat_bias_kernel(tc, x, w, b, wgo, offs, out):
         a = PASSES - 1
         spent = x_raw[a - 1][:].rearrange("p j c -> p (j c)").bitcast(BF16)
         low, high = columns(x_grouped[a - 1], 0, HALF), columns(spent, 0, HALF)
-        w_last, w_next = columns(x_grouped[a - 1], HALF, HALF + P), columns(x_grouped[a - 1], HALF + P, S)
+        w_last = columns(x_grouped[a - 1], HALF, HALF + P)
         interleave(scopy, high, x_raw[a][:, :, HALF:S])
         interleave(vcopy, low, x_raw[a][:, :, 0:HALF])
         interleave(vcopy, w_last, w_raw[0][a])
@@ -182,7 +189,7 @@ def tile_list_hscat_bias_kernel(tc, x, w, b, wgo, offs, out):
         quantize_x(a, HALF, S, high)
         multiply(late, a)
         units = [(1, 0, HALF), (1, HALF, S)]
-        spare = w_rows[1][:, 0 : 2 * PACK * P].bitcast(BF16)
+        spare = w_rows[1][:, PACK * P : 3 * PACK * P].bitcast(BF16)
 
         def prepare_second(copy, a0, a1, grouped):
             for a in range(a0, a1):
@@ -192,16 +199,20 @@ def tile_list_hscat_bias_kernel(tc, x, w, b, wgo, offs, out):
                 for a in range(a0, a1):
                     multiply(unit, a)
 
-        prepare_second(vcopy, 0, 1, w_next)
+        prepare_second(scopy, 0, 1, columns(w_second, SHARE, SHARE + P))
+        interleave(vcopy, columns(w_second, 0, SHARE), w_raw[1][1][:, :, 0:SHARE])
         y_first = keep.tile([P, HALF], F32, name="y_first")
         add_bias(first, y_first[:, 0:P], 0, P)
         add_bias(second, y_first[:, P:HALF], 0, P)
         place((0, 0, HALF), y_first[:])
-        prepare_second(scopy, 1, 2, columns(spare, 0, P))
-        prepare_second(scopy, 2, 3, columns(spare, P, HALF))
-        y_late = w_rows[1][:, 2 * PACK * P - EARLY : 2 * PACK * P - EARLY + HALF]
+        interleave(scopy, columns(w_second, SHARE, P), w_raw[1][1][:, :, SHARE:P])
+        quantize_w(1, 1, 2, columns(w_second, 0, P))
+        for unit in units:
+            multiply(unit, 1)
+        y_late = w_rows[1][:, 2 * PACK * P : 2 * PACK * P + HALF]
         add_bias(late, y_late[:, 0:EARLY], 0, EARLY)
-        prepare_second(scopy, 3, 4, columns(spare, HALF, HALF + P))
+        prepare_second(scopy, 2, 3, columns(spare, 0, P))
+        prepare_second(scopy, 3, 4, columns(spare, P, HALF))
         add_bias(late, y_late[:, EARLY:HALF], EARLY, HALF)
         place(late, y_late)
         for q in range(1, BLOCKS):

@@ -134,14 +134,13 @@ def tile_list_hscat_bias_kernel(tc, x, w, b, wgo, offs, out):
         nc.vector.memset(rows_in[:], 0.0)
         for a in range(PASSES - 1):
             load_w(0, a)
-        load_x(0)
         nc.sync.dma_start(
             out=rows_in[BIAS_ROW:P:QUAD, :].rearrange("u (q i) -> u q i", i=QUAD),
             in_=b.rearrange("(q u i) -> u q i", u=P // QUAD, i=QUAD),
         )
         half_rows = wgo.rearrange("p (v e) -> (p v) e", e=HALF)
         nc.sync.dma_start(out=rows_in[0 : P : GROUP // 2, :], in_=half_rows[0 : 2 * P : GROUP + 1, :])
-        for a in range(1, PASSES):
+        for a in range(PASSES):
             load_x(a)
         load_w(0, PASSES - 1)
         for q in range(1, BLOCKS):

@@ -28,6 +28,7 @@ QUAD = 32
 GROUP = 16
 BIAS_ROW = 4
 SHARE = 64
+X_LAST = 160
 
 
 def interleave(copy, grouped, raw):
@@ -64,8 +65,8 @@ def tile_list_hscat_bias_kernel(tc, x, w, b, wgo, offs, out):
             for q in range(BLOCKS)
         ]
         w_second = keep.tile([P, (P + SHARE) * PACK], BF16, align_bytes=64, name="w_second")
-        x_grouped = [keep.tile([P, S * PACK], BF16, align_bytes=64, name=f"x_grouped{a}") for a in range(PASSES - 1)]
-        w_first = [keep.tile([P, P * PACK], BF16, align_bytes=64, name=f"w_first{a}") for a in range(PASSES - 1)]
+        x_grouped = [keep.tile([P, S * PACK], BF16, align_bytes=64, name=f"x_grouped{a}") for a in range(PASSES)]
+        w_first = [keep.tile([P, P * PACK], BF16, align_bytes=64, name=f"w_first{a}") for a in range(PASSES)]
         vcopy, scopy = nc.vector.tensor_copy, nc.scalar.copy
 
         def load_x(a):
@@ -175,16 +176,16 @@ def tile_list_hscat_bias_kernel(tc, x, w, b, wgo, offs, out):
             for unit in (first, second, late):
                 multiply(unit, a)
         a = PASSES - 1
-        spent = x_raw[a - 1][:].rearrange("p j c -> p (j c)").bitcast(BF16)
-        low, high = columns(x_grouped[a - 1], 0, HALF), columns(spent, 0, HALF)
-        w_last = columns(x_grouped[a - 1], HALF, HALF + P)
+        low, high = columns(x_grouped[a], 0, HALF), columns(x_grouped[a], HALF, S)
+        interleave(scopy, columns(x_grouped[a], X_LAST, HALF), x_raw[a][:, :, X_LAST:HALF])
         interleave(scopy, high, x_raw[a][:, :, HALF:S])
-        interleave(vcopy, low, x_raw[a][:, :, 0:HALF])
-        interleave(vcopy, w_last, w_raw[0][a])
+        interleave(vcopy, columns(x_grouped[a], 0, X_LAST), x_raw[a][:, :, 0:X_LAST])
+        interleave(vcopy, w_first[a][:], w_raw[0][a])
         quantize_x(a, 0, HALF, low)
-        quantize_w(0, a, a + 1, w_last)
+        quantize_w(0, a, a + 1, w_first[a][:])
         multiply(first, a)
         multiply(second, a)
+        interleave(vcopy, columns(w_second, SHARE, SHARE + P), w_raw[1][0])
         quantize_x(a, HALF, S, high)
         multiply(late, a)
         units = [(1, 0, HALF), (1, HALF, S)]
@@ -198,7 +199,9 @@ def tile_list_hscat_bias_kernel(tc, x, w, b, wgo, offs, out):
                 for a in range(a0, a1):
                     multiply(unit, a)
 
-        prepare_second(scopy, 0, 1, columns(w_second, SHARE, SHARE + P))
+        quantize_w(1, 0, 1, columns(w_second, SHARE, SHARE + P))
+        for unit in units:
+            multiply(unit, 0)
         interleave(vcopy, columns(w_second, 0, SHARE), w_raw[1][1][:, :, 0:SHARE])
         y_first = keep.tile([P, HALF], F32, name="y_first")
         add_bias(first, y_first[:, 0:P], 0, P)

@@ -29,6 +29,7 @@ GROUP = 16
 BIAS_ROW = 4
 SHARE = 64
 X_LAST = 160
+BURST = 256
 
 
 def interleave(copy, grouped, raw):
@@ -49,15 +50,16 @@ def tile_list_hscat_bias_kernel(tc, x, w, b, wgo, offs, out):
         rows_in = keep.tile([P, HALF], F32, align_bytes=64, name="rows_in")
         turned = keep.tile([P, HALF], F32, align_bytes=64, name="turned")
         spread = keep.tile([P, S], F32, align_bytes=64, name="spread")
-        windows = [keep.tile([P, T], F32, name=f"window{i}") for i in range(WINDOWS)]
+        windows = [keep.tile([P, T], F32, align_bytes=BURST, name=f"window{i}") for i in range(WINDOWS)]
         x_codes = keep.tile([P, PASSES, S], U32, align_bytes=64, name="x_codes")
         x_scales = keep.tile([P, PASSES, S], U8, align_bytes=64, name="x_scales")
         w_codes = [keep.tile([P, PASSES, P], U32, align_bytes=64, name=f"w_codes{q}") for q in range(BLOCKS)]
         w_scales = [keep.tile([P, PASSES, P], U8, align_bytes=64, name=f"w_scales{q}") for q in range(BLOCKS)]
-        x_raw = [keep.tile([P, PACK, S], F32, align_bytes=64, name=f"x_raw{a}") for a in range(PASSES)]
+        x_raw = [keep.tile([P, PACK, S], F32, align_bytes=BURST, name=f"x_raw{a}") for a in range(PASSES)]
         gaps = [EARLY if q == 1 else 0 for q in range(BLOCKS)]
         w_rows = [
-            keep.tile([P, PASSES * PACK * P + gaps[q]], F32, align_bytes=64, name=f"w_rows{q}") for q in range(BLOCKS)
+            keep.tile([P, PASSES * PACK * P + gaps[q]], F32, align_bytes=BURST, name=f"w_rows{q}")
+            for q in range(BLOCKS)
         ]
         starts = [[a * PACK * P + (gaps[q] if a >= 2 else 0) for a in range(PASSES)] for q in range(BLOCKS)]
         w_raw = [

@@ -56,7 +56,7 @@ def tile_list_hscat_bias_kernel(tc, x, w, b, wgo, offs, out):
         w_codes = [keep.tile([P, PASSES, P], U32, align_bytes=64, name=f"w_codes{q}") for q in range(BLOCKS)]
         w_scales = [keep.tile([P, PASSES, P], U8, align_bytes=64, name=f"w_scales{q}") for q in range(BLOCKS)]
         x_raw = [keep.tile([P, PACK, S], F32, align_bytes=BURST, name=f"x_raw{a}") for a in range(PASSES)]
-        gaps = [EARLY if q == 1 else 0 for q in range(BLOCKS)]
+        gaps = [SHARE + EARLY if q == 1 else 0 for q in range(BLOCKS)]
         w_rows = [
             keep.tile([P, PASSES * PACK * P + gaps[q]], F32, align_bytes=BURST, name=f"w_rows{q}")
             for q in range(BLOCKS)
@@ -187,11 +187,11 @@ def tile_list_hscat_bias_kernel(tc, x, w, b, wgo, offs, out):
         quantize_w(0, a, a + 1, w_first[a][:])
         multiply(first, a)
         multiply(second, a)
-        interleave(vcopy, columns(w_second, SHARE, SHARE + P), w_raw[1][0])
+        interleave(vcopy, columns(w_second, 0, P), w_raw[1][0])
         quantize_x(a, HALF, S, high)
         multiply(late, a)
         units = [(1, 0, HALF), (1, HALF, S)]
-        spare = w_rows[1][:, PACK * P : 3 * PACK * P].bitcast(BF16)
+        spare = w_rows[1][:, PACK * P + SHARE : 3 * PACK * P + SHARE].bitcast(BF16)
 
         def prepare_second(copy, a0, a1, grouped):
             for a in range(a0, a1):
@@ -201,20 +201,22 @@ def tile_list_hscat_bias_kernel(tc, x, w, b, wgo, offs, out):
                 for a in range(a0, a1):
                     multiply(unit, a)
 
-        quantize_w(1, 0, 1, columns(w_second, SHARE, SHARE + P))
+        quantize_w(1, 0, 1, columns(w_second, 0, P))
         for unit in units:
             multiply(unit, 0)
-        interleave(vcopy, columns(w_second, 0, SHARE), w_raw[1][1][:, :, 0:SHARE])
-        y_first = keep.tile([P, HALF], F32, name="y_first")
-        add_bias(first, y_first[:, 0:P], 0, P)
-        add_bias(second, y_first[:, P:HALF], 0, P)
-        place((0, 0, HALF), y_first[:])
-        interleave(scopy, columns(w_second, SHARE, P), w_raw[1][1][:, :, SHARE:P])
-        quantize_w(1, 1, 2, columns(w_second, 0, P))
+        interleave(vcopy, columns(w_second, 2 * SHARE, SHARE + P), w_raw[1][1][:, :, SHARE:P])
+        y_first = keep.tile([P, P], F32, name="y_first")
+        add_bias(first, y_first[:], 0, P)
+        place(first, y_first[:])
+        interleave(scopy, columns(w_second, SHARE, 2 * SHARE), w_raw[1][1][:, :, 0:SHARE])
+        quantize_w(1, 1, 2, columns(w_second, SHARE, SHARE + P))
         for unit in units:
             multiply(unit, 1)
-        y_late = w_rows[1][:, 2 * PACK * P : 2 * PACK * P + HALF]
+        y_late = w_rows[1][:, 2 * PACK * P + SHARE : 2 * PACK * P + SHARE + HALF]
         add_bias(late, y_late[:, 0:EARLY], 0, EARLY)
+        y_second = w_rows[1][:, PACK * P + QUAD - P : PACK * P + QUAD]
+        add_bias(second, y_second, 0, P)
+        place(second, y_second)
         prepare_second(scopy, 2, 3, columns(spare, 0, P))
         prepare_second(scopy, 3, 4, columns(spare, P, HALF))
         add_bias(late, y_late[:, EARLY:HALF], EARLY, HALF)

@@ -29,7 +29,7 @@ GROUP = 16
 BIAS_ROW = 4
 SHARE = 64
 X_LAST = 160
-BURST = 256
+BURST = 512
 
 
 def interleave(copy, grouped, raw):

@@ -174,7 +174,8 @@ def tile_list_hscat_bias_kernel(tc, x, w, b, wgo, offs, out):
             prepare_first(a)
             interleave(scopy, columns(x_grouped[a], SPLIT, S), x_raw[a][:, :, SPLIT:S])
             interleave(vcopy, columns(x_grouped[a], 0, SPLIT), x_raw[a][:, :, 0:SPLIT])
-            quantize_x(a, 0, S, x_grouped[a][:])
+            for c in (0, SPLIT):
+                quantize_x(a, c, c + SPLIT, columns(x_grouped[a], c, c + SPLIT))
             for unit in (first, second, late):
                 multiply(unit, a)
         a = PASSES - 1

from contextlib import ExitStack

import concourse.mybir as mybir

K, M, T, S = 2048, 1024, 1024, 512
FLOPS = 2 * K * M * S

F32 = mybir.dt.float32
BF16 = mybir.dt.bfloat16
U32 = mybir.dt.uint32
U16 = mybir.dt.uint16
U8 = mybir.dt.uint8
FP8X4 = mybir.dt.float8_e4m3fn_x4
IDENTITY = mybir.ActivationFunctionType.Identity
MULT = mybir.AluOpType.mult

P = 128
PACK = 4
K_PASS = P * PACK
PASSES = K // K_PASS
BLOCKS = M // P
HALF = S // 2
WINDOWS = 6
HALVED = 3
SPLIT = 256
EARLY = 192
QUAD = 32
GROUP = 16
BIAS_ROW = 4
SHARE = 64
X_LAST = 160
BURST = 512


def interleave(copy, grouped, raw):
    copy(
        out=grouped.rearrange("p (c i j) -> p c j i", i=4, j=PACK),
        in_=raw.rearrange("p j (c i) -> p c j i", i=4),
    )


def tile_list_hscat_bias_kernel(tc, x, w, b, wgo, offs, out):
    nc = tc.nc
    with ExitStack() as ctx:
        keep = ctx.enter_context(tc.tile_pool(name="keep", bufs=1))
        psum = ctx.enter_context(tc.psum_pool(name="psum", bufs=8))

        offsets = keep.tile([P, S // 16], U16, name="offsets")
        weights = keep.tile([P, S], F32, align_bytes=64, name="weights")
        rows_in = keep.tile([P, HALF], F32, align_bytes=64, name="rows_in")
        turned = keep.tile([P, HALF], F32, align_bytes=64, name="turned")
        spread = keep.tile([P, S], F32, align_bytes=64, name="spread")
        windows = [keep.tile([P, T], F32, align_bytes=BURST, name=f"window{i}") for i in range(WINDOWS)]
        x_codes = keep.tile([P, PASSES, S], U32, align_bytes=64, name="x_codes")
        x_scales = keep.tile([P, PASSES, S], U8, align_bytes=64, name="x_scales")
        w_codes = [keep.tile([P, PASSES, P], U32, align_bytes=64, name=f"w_codes{q}") for q in range(BLOCKS)]
        w_scales = [keep.tile([P, PASSES, P], U8, align_bytes=64, name=f"w_scales{q}") for q in range(BLOCKS)]
        x_raw = [keep.tile([P, PACK, S], F32, align_bytes=BURST, name=f"x_raw{a}") for a in range(PASSES)]
        gaps = [SHARE + EARLY if q == 1 else 0 for q in range(BLOCKS)]
        w_rows = [
            keep.tile([P, PASSES * PACK * P + gaps[q]], F32, align_bytes=BURST, name=f"w_rows{q}")
            for q in range(BLOCKS)
        ]
        starts = [[a * PACK * P + (gaps[q] if a >= 2 else 0) for a in range(PASSES)] for q in range(BLOCKS)]
        w_raw = [
            [w_rows[q][:, i : i + PACK * P].rearrange("p (j c) -> p j c", j=PACK) for i in starts[q]]
            for q in range(BLOCKS)
        ]
        w_second = keep.tile([P, (P + SHARE) * PACK], BF16, align_bytes=64, name="w_second")
        x_grouped = [keep.tile([P, S * PACK], BF16, align_bytes=64, name=f"x_grouped{a}") for a in range(PASSES)]
        w_first = [keep.tile([P, P * PACK], BF16, align_bytes=64, name=f"w_first{a}") for a in range(PASSES)]
        vcopy, scopy = nc.vector.tensor_copy, nc.scalar.copy

        def load_x(a):
            rows = x[a * K_PASS : (a + 1) * K_PASS, :]
            nc.sync.dma_start(out=x_raw[a][:], in_=rows.rearrange("(p j) c -> p j c", j=PACK))

        def load_w(q, a):
            rows = w[a * K_PASS : (a + 1) * K_PASS, q * P : (q + 1) * P]
            queue = nc.scalar if q == 0 and a < PASSES - 1 else nc.sync
            queue.dma_start(out=w_raw[q][a], in_=rows.rearrange("(p j) c -> p j c", j=PACK))

        def quantize_x(a, c0, c1, grouped):
            nc.vector.quantize_mx(
                out=x_codes[:, a, c0:c1].bitcast(FP8X4), scales=x_scales[:, a, c0:c1], in_=grouped
            )

        def quantize_w(q, a0, a1, grouped):
            nc.vector.quantize_mx(
                out=w_codes[q][:, a0:a1, :].rearrange("p a c -> p (a c)").bitcast(FP8X4),
                scales=w_scales[q][:, a0:a1, :].rearrange("p a c -> p (a c)"),
                in_=grouped,
            )

        accs = {}

        def multiply(unit, a):
            q, c0, c1 = unit
            if a == 0:
                accs[unit] = psum.tile([P, S], F32, name="acc")
            nc.tensor.matmul_mx(
                out=accs[unit][:, 0 : c1 - c0],
                lhsT=w_codes[q][:, a, :].bitcast(FP8X4),
                lhsT_scale=w_scales[q][:, a, :],
                rhs=x_codes[:, a, c0:c1].bitcast(FP8X4),
                rhs_scale=x_scales[:, a, c0:c1],
                start=(a == 0),
                stop=(a == PASSES - 1),
            )

        def bias_of(q):
            return turned[:, q * QUAD + BIAS_ROW : q * QUAD + BIAS_ROW + 1]

        def place(unit, y):
            q, c0, c1 = unit
            nc.vector.tensor_tensor(
                windows[q % WINDOWS][:].indirect(offsets[:, c0 // 16 : c1 // 16]),
                y,
                weights[:, c0:c1],
                MULT,
            )
            if c1 == S:
                nc.sync.dma_start(out=out[q * P : (q + 1) * P, :], in_=windows[q % WINDOWS][:])

        def add_bias(unit, y, i0, i1):
            nc.scalar.activation(out=y, in_=accs[unit][:, i0:i1], func=IDENTITY, bias=bias_of(unit[0]))

        def place_on(unit, room):
            q, c0, c1 = unit
            add_bias(unit, room[:, 0 : c1 - c0], 0, c1 - c0)
            place(unit, room[:, 0 : c1 - c0])

        def place_own(unit):
            q, c0, c1 = unit
            place_on(unit, keep.tile([P, c1 - c0], F32, name=f"y{q}_{c0}"))

        nc.vector.memset(rows_in[:], 0.0)
        for a in range(PASSES - 1):
            load_w(0, a)
        nc.sync.dma_start(
            out=rows_in[BIAS_ROW:P:QUAD, :].rearrange("u (q i) -> u q i", i=QUAD),
            in_=b.rearrange("(q u i) -> u q i", u=P // QUAD, i=QUAD),
        )
        half_rows = wgo.rearrange("p (v e) -> (p v) e", e=HALF)
        nc.sync.dma_start(out=rows_in[0 : P : GROUP // 2, :], in_=half_rows[0 : 2 * P : GROUP + 1, :])
        for a in range(PASSES):
            load_x(a)
        load_w(0, PASSES - 1)
        for q in range(1, BLOCKS):
            for a in range(PASSES):
                if (q, a) == (1, 2):
                    nc.sync.dma_start(offsets[:], offs)
                load_w(q, a)
        for i in range(WINDOWS):
            nc.vector.memset(windows[i][:], 0.0)

        nc.vector.transpose(turned[:], rows_in[:])
        heads = turned[:].rearrange("p (g v r) -> p v g r", v=2, r=GROUP // 2)[:, :, :, 0:1]
        vcopy(
            out=spread[:].rearrange("p (v g r) -> p v g r", v=2, r=GROUP),
            in_=heads.to_broadcast([P, 2, HALF // GROUP, GROUP]),
        )
        nc.vector.transpose(weights[:], spread[:])
        first, second, late = (0, 0, P), (0, P, HALF), (0, HALF, S)

        def prepare_first(a):
            interleave(scopy, w_first[a][:], w_raw[0][a])
            quantize_w(0, a, a + 1, w_first[a][:])

        def columns(grouped, c0, c1):
            return grouped[:, c0 * PACK : c1 * PACK]

        for a in range(PASSES - 1):
            prepare_first(a)
            interleave(scopy, columns(x_grouped[a], SPLIT, S), x_raw[a][:, :, SPLIT:S])
            interleave(vcopy, columns(x_grouped[a], 0, SPLIT), x_raw[a][:, :, 0:SPLIT])
            for c in (0, SPLIT):
                quantize_x(a, c, c + SPLIT, columns(x_grouped[a], c, c + SPLIT))
            for unit in (first, second, late):
                multiply(unit, a)
        a = PASSES - 1
        low, high = columns(x_grouped[a], 0, HALF), columns(x_grouped[a], HALF, S)
        interleave(scopy, columns(x_grouped[a], X_LAST, HALF), x_raw[a][:, :, X_LAST:HALF])
        interleave(scopy, high, x_raw[a][:, :, HALF:S])
        interleave(vcopy, columns(x_grouped[a], 0, X_LAST), x_raw[a][:, :, 0:X_LAST])
        interleave(vcopy, w_first[a][:], w_raw[0][a])
        quantize_x(a, 0, HALF, low)
        quantize_w(0, a, a + 1, w_first[a][:])
        multiply(first, a)
        multiply(second, a)
        interleave(vcopy, columns(w_second, 0, P), w_raw[1][0])
        quantize_x(a, HALF, S, high)
        multiply(late, a)
        units = [(1, 0, HALF), (1, HALF, S)]
        spare = w_rows[1][:, PACK * P + SHARE : 3 * PACK * P + SHARE].bitcast(BF16)

        def prepare_second(copy, a0, a1, grouped):
            for a in range(a0, a1):
                interleave(copy, columns(grouped, (a - a0) * P, (a - a0 + 1) * P), w_raw[1][a])
            quantize_w(1, a0, a1, grouped)
            for unit in units:
                for a in range(a0, a1):
                    multiply(unit, a)

        quantize_w(1, 0, 1, columns(w_second, 0, P))
        for unit in units:
            multiply(unit, 0)
        interleave(vcopy, columns(w_second, 2 * SHARE, SHARE + P), w_raw[1][1][:, :, SHARE:P])
        y_first = keep.tile([P, P], F32, name="y_first")
        add_bias(first, y_first[:], 0, P)
        place(first, y_first[:])
        interleave(scopy, columns(w_second, SHARE, 2 * SHARE), w_raw[1][1][:, :, 0:SHARE])
        quantize_w(1, 1, 2, columns(w_second, SHARE, SHARE + P))
        for unit in units:
            multiply(unit, 1)
        y_late = w_rows[1][:, 2 * PACK * P + SHARE : 2 * PACK * P + SHARE + HALF]
        add_bias(late, y_late[:, 0:EARLY], 0, EARLY)
        y_second = w_rows[1][:, PACK * P + QUAD - P : PACK * P + QUAD]
        add_bias(second, y_second, 0, P)
        place(second, y_second)
        prepare_second(scopy, 2, 3, columns(spare, 0, P))
        prepare_second(scopy, 3, 4, columns(spare, P, HALF))
        add_bias(late, y_late[:, EARLY:HALF], EARLY, HALF)
        place(late, y_late)
        for q in range(1, BLOCKS):
            if q > 1:
                units = [(q, 0, HALF), (q, HALF, S)] if q < HALVED else [(q, 0, S)]
                step = PASSES if HALVED < q < BLOCKS - 1 else 2
                for a0 in range(0, PASSES, step):
                    for a in range(a0, a0 + step):
                        interleave(scopy, columns(spare, a * P, (a + 1) * P), w_raw[q][a])
                    quantize_w(q, a0, a0 + step, columns(spare, a0 * P, (a0 + step) * P))
                    for unit in units:
                        for a in range(a0, a0 + step):
                            multiply(unit, a)
                place_on(waiting, w_rows[q][:, 2 * PACK * P : 3 * PACK * P])
            for unit in units[:-1]:
                place_own(unit)
            waiting = units[-1]
        place_own(waiting)
